import numpy as np
import ml_dtypes


def mxq(x, axis, fmt="e4m3"):
    dtype, down = {"e4m3": (ml_dtypes.float8_e4m3fn, 7), "e5m2": (ml_dtypes.float8_e5m2, 14)}[fmt]
    v = np.moveaxis(np.asarray(x, np.float32).astype(ml_dtypes.bfloat16).astype(np.float64), axis, -1)
    blocks = v.reshape(v.shape[:-1] + (-1, 32))
    amax = np.abs(blocks).max(-1, keepdims=True)
    byte = np.maximum(np.where(amax > 0, np.frexp(amax)[1] - 1 + 127, 0) - down, 1)
    scale = np.exp2(byte - 127.0)
    codes = (blocks / scale).astype(np.float32).astype(dtype).astype(np.float64)
    return np.moveaxis((codes * scale).reshape(v.shape), -1, axis)


WIDE = False


def mx_kscale(k):
    if not WIDE:
        return np.ones(k)
    levels = np.array([10, -10, 5, -5, 0])
    if k % 512:
        return np.exp2(np.random.permutation(np.resize(levels, k // 32))).repeat(32)
    a = np.empty((k // 512, 16))
    for p in range(k // 512):
        a[p, :8] = np.random.permutation(np.resize(levels, 8))
        for g in range(8):
            far = levels[np.abs(levels - a[p, g]) >= 10]
            a[p, g + 8] = far[np.random.randint(len(far))]
    return np.exp2(a.ravel()).repeat(32)


def f64(x):
    return np.asarray(x).astype(np.float64)


def striped(idx):
    return np.tile(idx.reshape(-1, 16).T, (8, 1)).astype(np.uint16)


def unstriped(offs):
    return offs[:16].T.reshape(-1).astype(np.int64)


E2M1 = np.array([0.0, 0.5, 1.0, 1.5, 2.0, 3.0, 4.0, 6.0, -0.0, -0.5, -1.0, -1.5, -2.0, -3.0, -4.0, -6.0])


def pack_weight(w, fmt):
    k, n = w.shape
    w = f64(np.asarray(w, np.float32).astype(ml_dtypes.bfloat16)).reshape(k // 32, 32, n)
    amax = np.abs(w).max(1)
    if fmt == "e4m3":
        byte = np.frexp(amax)[1] - 1 + 127 - 7
    else:
        mant, ex = np.frexp(amax / 6.0)
        byte = np.where(mant > 0.5, ex, ex - 1) + 127
    byte = np.clip(np.where(amax > 0, byte, 1), 1, 254)
    scaled = (w * np.exp2(127.0 - byte)[:, None, :]).reshape(k, n).astype(np.float32)
    by_word = np.ascontiguousarray(scaled.reshape(k // 512, 128, 4, n).transpose(0, 1, 3, 2))
    if fmt == "e4m3":
        words = by_word.astype(ml_dtypes.float8_e4m3fn).view(np.uint8)
    else:
        c = by_word.astype(ml_dtypes.float4_e2m1fn).view(np.uint8) & 0xF
        words = (c[..., 0::2] | (c[..., 1::2] << 4)).reshape(k // 512, 128, 2 * n)
    return np.ascontiguousarray(words), np.ascontiguousarray(byte.astype(np.uint8).reshape(k // 512, 16, n))


def unpack_weight(words, scales, fmt):
    g, _, n = scales.shape
    words = np.ascontiguousarray(words).reshape(g, 128, n, -1)
    if fmt == "e4m3":
        vals = words.view(ml_dtypes.float8_e4m3fn).astype(np.float64)
    else:
        nib = np.empty((g, 128, n, 4), np.uint8)
        nib[..., 0::2] = words & 0xF
        nib[..., 1::2] = words >> 4
        vals = E2M1[nib]
    vals = vals * np.repeat(np.exp2(scales.astype(np.float64) - 127.0), 8, axis=1)[..., None]
    return vals.transpose(0, 1, 3, 2).reshape(g * 512, n)


def gelu(v):
    return 0.5 * v * (1.0 + np.tanh(np.sqrt(2.0 / np.pi) * (v + 0.044715 * v**3)))


def striped8(idx):
    return np.concatenate([v.reshape(-1, 16).T for v in idx]).astype(np.uint16)


def unstriped8(offs):
    return np.stack([offs[16 * g:16 * g + 16].T.reshape(-1) for g in range(8)]).astype(np.int64)


def heads(xT, wgt, idx8):
    k = np.arange(xT.shape[0])
    return wgt[k // 4 % 128] * xT[k[:, None], idx8[k % 512 // 64]]


K, T, S, H, N, G, P = 1024, 2048, 1024, 1024, 512, 8, 16

def setup_inputs():
    n = np.random.standard_normal
    s = mx_kscale(K)[:, None]
    u = mx_kscale(H)[:, None]
    xT = (n((K, T)) * s).astype(np.float32)
    wgt = np.repeat(np.random.uniform(0.5, 2.0, (G, S)), P, axis=0).astype(np.float32)
    offs = striped8(np.stack([np.random.permutation(T)[:S] for _ in range(G)]))
    we = (n((K, H)) / np.sqrt(K) / s * u.T).astype(np.float32)
    wo = (n((K, H)) / np.sqrt(K) / s * u.T).astype(np.float32)
    wd_words, wd_scales = pack_weight(n((H, N)) / np.sqrt(H) / u, "e2m1")
    bias = (0.5 * n(N)).astype(np.float32)
    return {"xT": xT, "wgt": wgt, "offs": offs, "we": we, "wo": wo,
            "wd_words": wd_words, "wd_scales": wd_scales, "bias": bias}

def reference(xT, wgt, offs, we, wo, wd_words, wd_scales, bias):
    xg = heads(f64(xT), f64(wgt), unstriped8(offs))
    xq = mxq(xg, 0, "e4m3")
    even = mxq(f64(we), 0, "e4m3").T @ xq
    odd = mxq(f64(wo), 0, "e4m3").T @ xq
    h = np.sqrt(np.square(even) + np.square(odd))
    wd = unpack_weight(wd_words, wd_scales, "e2m1")
    y = wd.T @ mxq(h, 0, "e4m3")
    return y + f64(bias)[:, None]

@@ -1,0 +1,232 @@
+from contextlib import ExitStack
+
+import concourse.mybir as mybir
+
+K, T, S, H, N = 1024, 2048, 1024, 1024, 512
+FLOPS = 2 * (2 * K * H * S + H * N * S)
+
+F32 = mybir.dt.float32
+BF16 = mybir.dt.bfloat16
+I32 = mybir.dt.int32
+U32 = mybir.dt.uint32
+U16 = mybir.dt.uint16
+U8 = mybir.dt.uint8
+FP8X4 = mybir.dt.float8_e4m3fn_x4
+FP4X4 = mybir.dt.float4_e2m1fn_x4
+ACT = mybir.ActivationFunctionType
+ALU = mybir.AluOpType
+
+P = 128
+PACK = 4
+KP = P * PACK
+W = 512
+
+
+def tile_list_deformable_texture_energy_kernel(tc, xT, wgt, offs, we, wo, wd_words, wd_scales, bias, out):
+    nc = tc.nc
+    with ExitStack() as ctx:
+        lists = ctx.enter_context(tc.tile_pool(name="lists", bufs=1))
+        keep = ctx.enter_context(tc.tile_pool(name="keep", bufs=1))
+        ring = ctx.enter_context(tc.tile_pool(name="ring", bufs=2))
+        psum = ctx.enter_context(tc.psum_pool(name="psum", bufs=1))
+
+        offsets = lists.tile([P, S // 16], U16, name="offsets")
+        nc.sync.dma_start(offsets[:], offs)
+
+        wd_plane = keep.tile([P, 2, N], U8, name="wd_plane", align_bytes=64)
+        nc.gpsimd.memset(wd_plane[:].rearrange("p a n -> p (a n)").bitcast(I32), 0)
+        for q in range(4):
+            nc.gpsimd.dma_start(
+                wd_plane[32 * q : 32 * q + 4, :, :].bitcast(I32),
+                wd_scales[:, 4 * q : 4 * q + 4, :].rearrange("a r n -> r a n").bitcast(I32),
+            )
+
+        warm = keep.tile([P, 2], F32, name="warm")
+        nc.vector.memset(warm[:, 0:1], 1.0)
+        nc.scalar.activation(warm[:, 1:2], warm[:, 0:1], ACT.Sqrt)
+
+        planes = {}
+        gains = {}
+        raws = {}
+        small = {}
+
+        def load_plane(a, i):
+            planes[a, i] = ring.tile([P, T], F32, name="plane%d%d" % (a, i), tag="plane%d%d" % (a, i), bufs=1, align_bytes=64)
+            rows = xT[KP * a : KP * (a + 1), :].rearrange("(p i) t -> p i t", i=PACK)
+            nc.sync.dma_start(planes[a, i][:], rows[:, i, :])
+
+        def load_gain(hf):
+            gains[hf] = keep.tile([P, W], F32, name="gain%d" % hf)
+            nc.sync.dma_start(gains[hf][:], wgt[:, W * hf : W * (hf + 1)])
+
+        def load_filter(f, b, a, tag="raw", bufs=1):
+            raws[f, b, a] = ring.tile([P, PACK, W], F32, name="raw", tag=tag, bufs=bufs, align_bytes=64)
+            rows = (we, wo)[f][KP * a : KP * (a + 1), W * b : W * (b + 1)]
+            nc.sync.dma_start(raws[f, b, a][:], rows.rearrange("(p i) c -> p i c", i=PACK))
+
+        def load_small():
+            small["wd"] = keep.tile([P, 2, 2 * N], U8, name="wd_codes", align_bytes=64)
+            nc.sync.dma_start(small["wd"][:].bitcast(I32), wd_words.rearrange("a p c -> p a c").bitcast(I32))
+            small["bias"] = keep.tile([P, N // P], F32, name="bias_cols")
+            with nc.allow_non_contiguous_dma(reason="one bias value a partition"):
+                nc.sync.dma_start(small["bias"][:], bias.rearrange("(u p) -> p u", p=P))
+
+        def code_tiles(name):
+            codes = keep.tile([P, W], U32, name=name + "c", align_bytes=64)
+            scales = keep.tile([P, W], U8, name=name + "s", align_bytes=64)
+            return codes, scales
+
+        def quantise(pair, grouped, lo=0, hi=W):
+            nc.vector.quantize_mx(
+                out=pair[0][:, lo:hi].bitcast(FP8X4), scales=pair[1][:, lo:hi], in_=grouped[:, PACK * lo : PACK * hi]
+            )
+
+        xq = {}
+        wq = {}
+        hq = {}
+        picked = {}
+        squares = {}
+        hgrp = {}
+
+        def gather(hf, a, i):
+            if i == 0:
+                picked[hf, a] = ring.tile([P, PACK, W], F32, name="picked", tag="wide", bufs=8)
+            cut = offsets[:, hf * W // 16 : (hf + 1) * W // 16]
+            nc.vector.tensor_tensor(picked[hf, a][:, i, :], planes[a, i][:].indirect(cut), gains[hf][:], ALU.mult)
+
+        def weave_x(hf, a, share, tag="xgrp", bufs=2):
+            grouped = ring.tile([P, PACK * W], BF16, name="xgrp", tag=tag, bufs=bufs, align_bytes=64)
+            dst = grouped[:].rearrange("p (c j i) -> p c i j", j=4, i=PACK)
+            src = picked[hf, a][:].rearrange("p i (c j) -> p c i j", j=4)
+            if share > 0:
+                nc.vector.tensor_copy(dst[:, :share], src[:, :share])
+            if share < P:
+                nc.scalar.copy(dst[:, share:], src[:, share:])
+            xq[hf, a] = code_tiles("xq%d%d" % (hf, a))
+            quantise(xq[hf, a], grouped)
+
+        def weave_w(f, b, a, share, tag="wgrp", bufs=2):
+            grouped = ring.tile([P, PACK * W], BF16, name="wgrp", tag=tag, bufs=bufs, align_bytes=64)
+            dst = grouped[:].rearrange("p (t m i) -> p m i t", t=PACK, i=PACK)
+            src = raws[f, b, a][:].rearrange("p i (m t) -> p m i t", t=PACK)
+            if share > 0:
+                nc.vector.tensor_copy(dst[:, :, :, :share], src[:, :, :, :share])
+            if share < PACK:
+                nc.scalar.copy(dst[:, :, :, share:], src[:, :, :, share:])
+            wq[f, b, a] = code_tiles("wq%d%d%d" % (f, b, a))
+            quantise(wq[f, b, a], grouped)
+
+        def product(acc, still, t, moving):
+            for a in range(2):
+                nc.tensor.matmul_mx(
+                    acc[:],
+                    lhsT=still[a][0][:, P * t : P * (t + 1)].bitcast(FP8X4),
+                    lhsT_scale=still[a][1][:, P * t : P * (t + 1)],
+                    rhs=moving[a][0][:].bitcast(FP8X4),
+                    rhs_scale=moving[a][1][:],
+                    start=(a == 0),
+                    stop=(a == 1),
+                )
+
+        def respond(f, b, hf, turned=False, on_vector=()):
+            squares[f, b, hf] = ring.tile([P, PACK, W], F32, name="sq", tag="wide", bufs=8)
+            filt = [wq[f, b, a] for a in range(2)]
+            toks = [xq[hf, a] for a in range(2)]
+            for t in range(PACK):
+                acc = psum.tile([P, W], F32, name="acc", tag="acc", bufs=4)
+                if turned:
+                    product(acc, toks, t, filt)
+                else:
+                    product(acc, filt, t, toks)
+                if t in on_vector:
+                    plain = ring.tile([P, W], F32, name="plain", tag="result", bufs=4)
+                    nc.vector.tensor_copy(plain[:], acc[:])
+                    nc.vector.tensor_tensor(squares[f, b, hf][:, t, :], acc[:], plain[:], ALU.mult)
+                else:
+                    nc.scalar.activation(squares[f, b, hf][:, t, :], acc[:], ACT.Square)
+
+        def energy(b, hf, parts=1, tag=None):
+            grouped = ring.tile([P, PACK * W], BF16, name="hgrp", tag="hgrp", bufs=4, align_bytes=64)
+            hq[b, hf] = code_tiles("hq%d%d" % (b, hf))
+            step = W // parts
+            for lo in range(0, W, step):
+                total = ring.tile([P, PACK, step], F32, name="total", tag=tag[lo // step], bufs=1, align_bytes=64)
+                part = total[:]
+                nc.vector.tensor_tensor(part, squares[0, b, hf][:, :, lo : lo + step], squares[1, b, hf][:, :, lo : lo + step], ALU.add)
+                nc.scalar.activation(
+                    grouped[:, PACK * lo : PACK * (lo + step)].rearrange("p (c j t) -> p c t j", j=4, t=PACK),
+                    part.rearrange("p t (c j) -> p c t j", j=4),
+                    ACT.Sqrt,
+                )
+                quantise(hq[b, hf], grouped, lo, lo + step)
+
+
+        def codes_out(hf, on_scalar, lo=0, hi=W):
+            for u in range(N // P):
+                acc = psum.tile([P, W], F32, name="fin", tag="fin", bufs=4)
+                for b in range(2):
+                    nc.tensor.matmul_mx(
+                        acc[:],
+                        lhsT=small["wd"][:, b, 2 * P * u : 2 * P * (u + 1)].bitcast(FP4X4),
+                        lhsT_scale=wd_plane[:, b, P * u : P * (u + 1)],
+                        rhs=hq[b, hf][0][:].bitcast(FP8X4),
+                        rhs_scale=hq[b, hf][1][:],
+                        start=(b == 0),
+                        stop=(b == 1),
+                    )
+                result = ring.tile([P, W], F32, name="result", tag="result", bufs=4)
+                if u in on_scalar:
+                    nc.scalar.activation(result[:], acc[:], ACT.Identity, bias=small["bias"][:, u : u + 1])
+                else:
+                    nc.vector.tensor_scalar_add(result[:], acc[:], small["bias"][:, u : u + 1])
+                nc.sync.dma_start(out[P * u : P * (u + 1), W * hf : W * (hf + 1)], result[:])
+
+        load_gain(0)
+        load_plane(0, 0)
+        load_gain(1)
+        for i in range(1, PACK):
+            load_plane(0, i)
+        for i in range(3):
+            load_plane(1, i)
+        load_filter(0, 0, 0, "first", 1)
+        load_plane(1, 3)
+        load_filter(0, 0, 1, "once", 1)
+        for i in range(PACK):
+            gather(0, 0, i)
+            gather(1, 0, i)
+        load_filter(1, 0, 0, "plane00", 1)
+        load_filter(1, 0, 1, "plane01", 1)
+        load_filter(0, 1, 0, "plane02", 1)
+        load_filter(0, 1, 1, "plane03", 1)
+        weave_x(0, 0, 0)
+        weave_x(1, 0, 0)
+        for i in range(PACK):
+            gather(0, 1, i)
+            gather(1, 1, i)
+        load_filter(1, 1, 0, "plane10", 1)
+        load_filter(1, 1, 1, "plane11", 1)
+        load_small()
+        weave_w(0, 0, 0, 0)
+        weave_x(0, 1, 128)
+        weave_w(0, 0, 1, 0, "w1", 1)
+        weave_x(1, 1, 0, "once", 1)
+        weave_w(1, 0, 0, 4, "w1", 1)
+        weave_w(1, 0, 1, 4, "once", 1)
+        weave_w(0, 1, 0, 4)
+        weave_w(0, 1, 1, 4)
+        weave_w(1, 1, 0, 4)
+        weave_w(1, 1, 1, 4)
+        respond(0, 0, 0)
+        respond(0, 0, 1)
+        respond(1, 0, 0)
+        respond(1, 0, 1)
+        respond(0, 1, 0)
+        respond(0, 1, 1, False, ())
+        respond(1, 1, 0)
+        respond(1, 1, 1, False, ())
+        energy(0, 0, 1, ["plane11"])
+        energy(1, 0, 1, ["plane10"])
+        energy(0, 1, 1, ["plane12"])
+        energy(1, 1, 2, ["plane13", "plane03"])
+        codes_out(0, ())
+        codes_out(1, (1, 3))

@@ -35,11 +35,6 @@ def tile_list_deformable_texture_energy_kernel(tc, xT, wgt, offs, we, wo, wd_wor
 
         wd_plane = keep.tile([P, 2, N], U8, name="wd_plane", align_bytes=64)
         nc.gpsimd.memset(wd_plane[:].rearrange("p a n -> p (a n)").bitcast(I32), 0)
-        for q in range(4):
-            nc.gpsimd.dma_start(
-                wd_plane[32 * q : 32 * q + 4, :, :].bitcast(I32),
-                wd_scales[:, 4 * q : 4 * q + 4, :].rearrange("a r n -> r a n").bitcast(I32),
-            )
 
         warm = keep.tile([P, 2], F32, name="warm")
         nc.vector.memset(warm[:, 0:1], 1.0)
@@ -67,6 +62,11 @@ def tile_list_deformable_texture_energy_kernel(tc, xT, wgt, offs, we, wo, wd_wor
         def load_small():
             small["wd"] = keep.tile([P, 2, 2 * N], U8, name="wd_codes", align_bytes=64)
             nc.sync.dma_start(small["wd"][:].bitcast(I32), wd_words.rearrange("a p c -> p a c").bitcast(I32))
+            for q in range(4):
+                nc.sync.dma_start(
+                    wd_plane[32 * q : 32 * q + 4, :, :].bitcast(I32),
+                    wd_scales[:, 4 * q : 4 * q + 4, :].rearrange("a r n -> r a n").bitcast(I32),
+                )
             small["bias"] = keep.tile([P, N // P], F32, name="bias_cols")
             with nc.allow_non_contiguous_dma(reason="one bias value a partition"):
                 nc.sync.dma_start(small["bias"][:], bias.rearrange("(u p) -> p u", p=P))
@@ -76,9 +76,9 @@ def tile_list_deformable_texture_energy_kernel(tc, xT, wgt, offs, we, wo, wd_wor
             scales = keep.tile([P, W], U8, name=name + "s", align_bytes=64)
             return codes, scales
 
-        def quantise(pair, grouped, lo=0, hi=W):
+        def quantise(pair, grouped, lo=0, hi=W, base=0):
             nc.vector.quantize_mx(
-                out=pair[0][:, lo:hi].bitcast(FP8X4), scales=pair[1][:, lo:hi], in_=grouped[:, PACK * lo : PACK * hi]
+                out=pair[0][:, lo:hi].bitcast(FP8X4), scales=pair[1][:, lo:hi], in_=grouped[:, PACK * (lo - base) : PACK * (hi - base)]
             )
 
         xq = {}
@@ -90,7 +90,7 @@ def tile_list_deformable_texture_energy_kernel(tc, xT, wgt, offs, we, wo, wd_wor
 
         def gather(hf, a, i):
             if i == 0:
-                picked[hf, a] = ring.tile([P, PACK, W], F32, name="picked", tag="wide", bufs=8)
+                picked[hf, a] = ring.tile([P, PACK, W], F32, name="picked", tag="wide", bufs=7, align_bytes=64)
             cut = offsets[:, hf * W // 16 : (hf + 1) * W // 16]
             nc.vector.tensor_tensor(picked[hf, a][:, i, :], planes[a, i][:].indirect(cut), gains[hf][:], ALU.mult)
 
@@ -128,42 +128,42 @@ def tile_list_deformable_texture_energy_kernel(tc, xT, wgt, offs, we, wo, wd_wor
                     stop=(a == 1),
                 )
 
-        def respond(f, b, hf, turned=False, on_vector=()):
-            squares[f, b, hf] = ring.tile([P, PACK, W], F32, name="sq", tag="wide", bufs=8)
+        def respond(f, b, hf, turned=False, on_vector=(), ptag="result", pbufs=8, tag="wide", bufs=7):
+            squares[f, b, hf] = ring.tile([P, PACK, W], F32, name="sq", tag=tag, bufs=bufs, align_bytes=64)
             filt = [wq[f, b, a] for a in range(2)]
             toks = [xq[hf, a] for a in range(2)]
             for t in range(PACK):
-                acc = psum.tile([P, W], F32, name="acc", tag="acc", bufs=4)
+                acc = psum.tile([P, W], F32, name="acc", tag="acc", bufs=5)
                 if turned:
                     product(acc, toks, t, filt)
                 else:
                     product(acc, filt, t, toks)
                 if t in on_vector:
-                    plain = ring.tile([P, W], F32, name="plain", tag="result", bufs=4)
+                    plain = ring.tile([P, W], F32, name="plain", tag=ptag, bufs=pbufs, align_bytes=64)
                     nc.vector.tensor_copy(plain[:], acc[:])
                     nc.vector.tensor_tensor(squares[f, b, hf][:, t, :], acc[:], plain[:], ALU.mult)
                 else:
                     nc.scalar.activation(squares[f, b, hf][:, t, :], acc[:], ACT.Square)
 
-        def energy(b, hf, parts=1, tag=None):
-            grouped = ring.tile([P, PACK * W], BF16, name="hgrp", tag="hgrp", bufs=4, align_bytes=64)
-            hq[b, hf] = code_tiles("hq%d%d" % (b, hf))
-            step = W // parts
-            for lo in range(0, W, step):
-                total = ring.tile([P, PACK, step], F32, name="total", tag=tag[lo // step], bufs=1, align_bytes=64)
+        def energy(b, hf, lo, step, tag, gtag="hgrp", gbufs=3):
+            if lo == 0:
+                hq[b, hf] = code_tiles("hq%d%d" % (b, hf))
+            if True:
+                grouped = ring.tile([P, PACK * step], BF16, name="hgrp", tag=gtag, bufs=gbufs, align_bytes=64)
+                total = ring.tile([P, PACK, step], F32, name="total", tag=tag, bufs=1, align_bytes=64)
                 part = total[:]
                 nc.vector.tensor_tensor(part, squares[0, b, hf][:, :, lo : lo + step], squares[1, b, hf][:, :, lo : lo + step], ALU.add)
                 nc.scalar.activation(
-                    grouped[:, PACK * lo : PACK * (lo + step)].rearrange("p (c j t) -> p c t j", j=4, t=PACK),
+                    grouped[:].rearrange("p (c j t) -> p c t j", j=4, t=PACK),
                     part.rearrange("p t (c j) -> p c t j", j=4),
                     ACT.Sqrt,
                 )
-                quantise(hq[b, hf], grouped, lo, lo + step)
+                quantise(hq[b, hf], grouped, lo, lo + step, lo)
 
 
         def codes_out(hf, on_scalar, lo=0, hi=W):
             for u in range(N // P):
-                acc = psum.tile([P, W], F32, name="fin", tag="fin", bufs=4)
+                acc = psum.tile([P, W], F32, name="fin", tag="fin", bufs=3)
                 for b in range(2):
                     nc.tensor.matmul_mx(
                         acc[:],
@@ -174,20 +174,47 @@ def tile_list_deformable_texture_energy_kernel(tc, xT, wgt, offs, we, wo, wd_wor
                         start=(b == 0),
                         stop=(b == 1),
                     )
-                result = ring.tile([P, W], F32, name="result", tag="result", bufs=4)
+                result = ring.tile([P, W], F32, name="result", tag="result", bufs=8, align_bytes=64)
                 if u in on_scalar:
                     nc.scalar.activation(result[:], acc[:], ACT.Identity, bias=small["bias"][:, u : u + 1])
                 else:
                     nc.vector.tensor_scalar_add(result[:], acc[:], small["bias"][:, u : u + 1])
                 nc.sync.dma_start(out[P * u : P * (u + 1), W * hf : W * (hf + 1)], result[:])
 
+        def codes_part(hf, lo, step):
+            for pair in range(2):
+                acc = psum.tile([P, 2, step], F32, name="fin", tag="fin", bufs=3)
+                passes = [(b, v, c) for b in range(2) for v in range(2) for c in range(0, step, P)]
+                for b, v, c in passes:
+                    u = 2 * pair + v
+                    nc.tensor.matmul_mx(
+                        acc[:, v, c : c + P],
+                        lhsT=small["wd"][:, b, 2 * P * u : 2 * P * (u + 1)].bitcast(FP4X4),
+                        lhsT_scale=wd_plane[:, b, P * u : P * (u + 1)],
+                        rhs=hq[b, hf][0][:, lo + c : lo + c + P].bitcast(FP8X4),
+                        rhs_scale=hq[b, hf][1][:, lo + c : lo + c + P],
+                        start=((b, v, c) == passes[0]),
+                        stop=((b, v, c) == passes[-1]),
+                    )
+                result = ring.tile([P, 2, step], F32, name="result", tag="result", bufs=8, align_bytes=64)
+                for v in range(2):
+                    u = 2 * pair + v
+                    if pair == 1:
+                        nc.scalar.activation(result[:, v, :], acc[:, v, :], ACT.Identity, bias=small["bias"][:, u : u + 1])
+                    else:
+                        nc.vector.tensor_scalar_add(result[:, v, :], acc[:, v, :], small["bias"][:, u : u + 1])
+                rows = out[2 * P * pair : 2 * P * (pair + 1), W * hf + lo : W * hf + lo + step]
+                nc.sync.dma_start(rows.rearrange("(v p) j -> p v j", p=P), result[:])
+
         load_gain(0)
         load_plane(0, 0)
         load_gain(1)
-        for i in range(1, PACK):
-            load_plane(0, i)
-        for i in range(3):
-            load_plane(1, i)
+        load_plane(0, 1)
+        load_plane(0, 2)
+        load_plane(0, 3)
+        load_plane(1, 0)
+        load_plane(1, 1)
+        load_plane(1, 2)
         load_filter(0, 0, 0, "first", 1)
         load_plane(1, 3)
         load_filter(0, 0, 1, "once", 1)
@@ -200,33 +227,39 @@ def tile_list_deformable_texture_energy_kernel(tc, xT, wgt, offs, we, wo, wd_wor
         load_filter(0, 1, 1, "plane03", 1)
         weave_x(0, 0, 0)
         weave_x(1, 0, 0)
-        for i in range(PACK):
+        for i in range(3):
             gather(0, 1, i)
             gather(1, 1, i)
         load_filter(1, 1, 0, "plane10", 1)
         load_filter(1, 1, 1, "plane11", 1)
         load_small()
+        gather(0, 1, 3)
         weave_w(0, 0, 0, 0)
-        weave_x(0, 1, 128)
-        weave_w(0, 0, 1, 0, "w1", 1)
-        weave_x(1, 1, 0, "once", 1)
-        weave_w(1, 0, 0, 4, "w1", 1)
-        weave_w(1, 0, 1, 4, "once", 1)
+        weave_w(0, 0, 1, 0)
+        weave_x(0, 1, 128, "w1", 1)
+        gather(1, 1, 3)
+        weave_x(1, 1, 128, "once", 1)
+        weave_w(1, 0, 0, 0)
+        weave_w(1, 0, 1, 4)
         weave_w(0, 1, 0, 4)
         weave_w(0, 1, 1, 4)
         weave_w(1, 1, 0, 4)
-        weave_w(1, 1, 1, 4)
+        weave_w(1, 1, 1, 4, "first", 1)
         respond(0, 0, 0)
         respond(0, 0, 1)
         respond(1, 0, 0)
         respond(1, 0, 1)
         respond(0, 1, 0)
-        respond(0, 1, 1, False, ())
-        respond(1, 1, 0)
-        respond(1, 1, 1, False, ())
-        energy(0, 0, 1, ["plane11"])
-        energy(1, 0, 1, ["plane10"])
-        energy(0, 1, 1, ["plane12"])
-        energy(1, 1, 2, ["plane13", "plane03"])
+        respond(1, 1, 0, False, (), "result", 8, "plane00", 1)
+        energy(0, 0, 0, W, "first", "h0", 1)
+        energy(1, 0, 0, W, "plane10")
+        respond(0, 1, 1, False, (3,), "h0", 1)
+        respond(1, 1, 1, False, (), "h0", 1)
+        energy(0, 1, 0, W, "plane00")
+        energy(1, 1, 0, 256, "plane13")
+        energy(1, 1, 256, 128, "plane03")
+        energy(1, 1, 384, 128, "plane02")
         codes_out(0, ())
-        codes_out(1, (1, 3))
+        codes_part(1, 0, 256)
+        codes_part(1, 256, 128)
+        codes_part(1, 384, 128)

@@ -20,6 +20,7 @@ P = 128
 PACK = 4
 KP = P * PACK
 W = 512
+EVEN, ODD = 0, 1
 
 
 def tile_list_deformable_texture_energy_kernel(tc, xT, wgt, offs, we, wo, wd_words, wd_scales, bias, out):
@@ -27,239 +28,231 @@ def tile_list_deformable_texture_energy_kernel(tc, xT, wgt, offs, we, wo, wd_wor
     with ExitStack() as ctx:
         lists = ctx.enter_context(tc.tile_pool(name="lists", bufs=1))
         keep = ctx.enter_context(tc.tile_pool(name="keep", bufs=1))
-        ring = ctx.enter_context(tc.tile_pool(name="ring", bufs=2))
         psum = ctx.enter_context(tc.psum_pool(name="psum", bufs=1))
+
+        def slot(shape, dtype, tag, bufs=1):
+            return keep.tile(shape, dtype, name=tag, tag=tag, bufs=bufs, align_bytes=64)
 
         offsets = lists.tile([P, S // 16], U16, name="offsets")
         nc.sync.dma_start(offsets[:], offs)
 
-        wd_plane = keep.tile([P, 2, N], U8, name="wd_plane", align_bytes=64)
+        wd_plane = slot([P, 2, N], U8, "wd_plane")
         nc.gpsimd.memset(wd_plane[:].rearrange("p a n -> p (a n)").bitcast(I32), 0)
 
-        warm = keep.tile([P, 2], F32, name="warm")
+        warm = slot([P, 2], F32, "warm")
         nc.vector.memset(warm[:, 0:1], 1.0)
         nc.scalar.activation(warm[:, 1:2], warm[:, 0:1], ACT.Sqrt)
 
-        planes = {}
-        gains = {}
-        raws = {}
-        small = {}
+        planes, gains, raws, small = {}, {}, {}, {}
+        xq, wq, hq, picked, squares = {}, {}, {}, {}, {}
 
         def load_plane(a, i):
-            planes[a, i] = ring.tile([P, T], F32, name="plane%d%d" % (a, i), tag="plane%d%d" % (a, i), bufs=1, align_bytes=64)
+            planes[a, i] = slot([P, T], F32, "plane%d%d" % (a, i))
             rows = xT[KP * a : KP * (a + 1), :].rearrange("(p i) t -> p i t", i=PACK)
             nc.sync.dma_start(planes[a, i][:], rows[:, i, :])
 
         def load_gain(hf):
-            gains[hf] = keep.tile([P, W], F32, name="gain%d" % hf)
+            gains[hf] = slot([P, W], F32, "gain%d" % hf)
             nc.sync.dma_start(gains[hf][:], wgt[:, W * hf : W * (hf + 1)])
 
-        def load_filter(f, b, a, tag="raw", bufs=1):
-            raws[f, b, a] = ring.tile([P, PACK, W], F32, name="raw", tag=tag, bufs=bufs, align_bytes=64)
-            rows = (we, wo)[f][KP * a : KP * (a + 1), W * b : W * (b + 1)]
-            nc.sync.dma_start(raws[f, b, a][:], rows.rearrange("(p i) c -> p i c", i=PACK))
+        def load_filter(f, a, blocks, tag):
+            lo, hi = W * blocks[0], W * (blocks[-1] + 1)
+            raw = slot([P, PACK, hi - lo], F32, tag)
+            rows = (we, wo)[f][KP * a : KP * (a + 1), lo:hi]
+            nc.sync.dma_start(raw[:], rows.rearrange("(p i) c -> p i c", i=PACK))
+            for b in blocks:
+                raws[f, b, a] = raw[:, :, W * b - lo : W * (b + 1) - lo]
 
         def load_small():
-            small["wd"] = keep.tile([P, 2, 2 * N], U8, name="wd_codes", align_bytes=64)
+            small["wd"] = slot([P, 2, 2 * N], U8, "wd_codes")
             nc.sync.dma_start(small["wd"][:].bitcast(I32), wd_words.rearrange("a p c -> p a c").bitcast(I32))
             for q in range(4):
                 nc.sync.dma_start(
                     wd_plane[32 * q : 32 * q + 4, :, :].bitcast(I32),
                     wd_scales[:, 4 * q : 4 * q + 4, :].rearrange("a r n -> r a n").bitcast(I32),
                 )
-            small["bias"] = keep.tile([P, N // P], F32, name="bias_cols")
+            small["bias"] = slot([P, N // P], F32, "bias_cols")
             with nc.allow_non_contiguous_dma(reason="one bias value a partition"):
                 nc.sync.dma_start(small["bias"][:], bias.rearrange("(u p) -> p u", p=P))
 
-        def code_tiles(name):
-            codes = keep.tile([P, W], U32, name=name + "c", align_bytes=64)
-            scales = keep.tile([P, W], U8, name=name + "s", align_bytes=64)
+        def quantise(grouped, name):
+            width = grouped.shape[1] // PACK
+            codes = slot([P, width], U32, name + "c")
+            scales = slot([P, width], U8, name + "s")
+            nc.vector.quantize_mx(out=codes[:].bitcast(FP8X4), scales=scales[:], in_=grouped[:])
             return codes, scales
 
-        def quantise(pair, grouped, lo=0, hi=W, base=0):
-            nc.vector.quantize_mx(
-                out=pair[0][:, lo:hi].bitcast(FP8X4), scales=pair[1][:, lo:hi], in_=grouped[:, PACK * (lo - base) : PACK * (hi - base)]
-            )
+        def load_gains():
+            gains["all"] = slot([P, S], F32, "gains")
+            nc.sync.dma_start(gains["all"][:, :W], wgt[:, :W])
 
-        xq = {}
-        wq = {}
-        hq = {}
-        picked = {}
-        squares = {}
-        hgrp = {}
+        def load_gains_rest():
+            nc.sync.dma_start(gains["all"][:, W:], wgt[:, W:])
+
+        def gather_span(a, i, lo, hi):
+            if (i, lo) == (0, 0):
+                picked[a] = slot([P, PACK, S], F32, "pickedall%d" % a)
+                for hf in range(2):
+                    picked[hf, a] = picked[a][:, :, W * hf : W * (hf + 1)]
+            cut = offsets[:, lo // 16 : hi // 16]
+            nc.vector.tensor_tensor(picked[a][:, i, lo:hi], planes[a, i][:].indirect(cut), gains["all"][:, lo:hi], ALU.mult)
 
         def gather(hf, a, i):
             if i == 0:
-                picked[hf, a] = ring.tile([P, PACK, W], F32, name="picked", tag="wide", bufs=7, align_bytes=64)
+                picked[hf, a] = slot([P, PACK, W], F32, "picked%d%d" % (hf, a))
             cut = offsets[:, hf * W // 16 : (hf + 1) * W // 16]
             nc.vector.tensor_tensor(picked[hf, a][:, i, :], planes[a, i][:].indirect(cut), gains[hf][:], ALU.mult)
 
         def weave_x(hf, a, share, tag="xgrp", bufs=2):
-            grouped = ring.tile([P, PACK * W], BF16, name="xgrp", tag=tag, bufs=bufs, align_bytes=64)
+            grouped = slot([P, PACK * W], BF16, tag, bufs)
             dst = grouped[:].rearrange("p (c j i) -> p c i j", j=4, i=PACK)
             src = picked[hf, a][:].rearrange("p i (c j) -> p c i j", j=4)
             if share > 0:
                 nc.vector.tensor_copy(dst[:, :share], src[:, :share])
             if share < P:
                 nc.scalar.copy(dst[:, share:], src[:, share:])
-            xq[hf, a] = code_tiles("xq%d%d" % (hf, a))
-            quantise(xq[hf, a], grouped)
+            xq[hf, a] = quantise(grouped, "xq%d%d" % (hf, a))
 
-        def weave_w(f, b, a, share, tag="wgrp", bufs=2):
-            grouped = ring.tile([P, PACK * W], BF16, name="wgrp", tag=tag, bufs=bufs, align_bytes=64)
-            dst = grouped[:].rearrange("p (t m i) -> p m i t", t=PACK, i=PACK)
-            src = raws[f, b, a][:].rearrange("p i (m t) -> p m i t", t=PACK)
-            if share > 0:
-                nc.vector.tensor_copy(dst[:, :, :, :share], src[:, :, :, :share])
-            if share < PACK:
-                nc.scalar.copy(dst[:, :, :, share:], src[:, :, :, share:])
-            wq[f, b, a] = code_tiles("wq%d%d%d" % (f, b, a))
-            quantise(wq[f, b, a], grouped)
+        def weave_w(f, b, a, copy, tag="wgrp", bufs=2):
+            grouped = slot([P, PACK * W], BF16, tag, bufs)
+            copy(
+                grouped[:].rearrange("p (t m i) -> p m i t", t=PACK, i=PACK),
+                raws[f, b, a].rearrange("p i (m t) -> p m i t", t=PACK),
+            )
+            wq[f, b, a] = quantise(grouped, "wq%d%d%d" % (f, b, a))
 
-        def product(acc, still, t, moving):
-            for a in range(2):
-                nc.tensor.matmul_mx(
-                    acc[:],
-                    lhsT=still[a][0][:, P * t : P * (t + 1)].bitcast(FP8X4),
-                    lhsT_scale=still[a][1][:, P * t : P * (t + 1)],
-                    rhs=moving[a][0][:].bitcast(FP8X4),
-                    rhs_scale=moving[a][1][:],
-                    start=(a == 0),
-                    stop=(a == 1),
-                )
-
-        def respond(f, b, hf, turned=False, on_vector=(), ptag="result", pbufs=8, tag="wide", bufs=7):
-            squares[f, b, hf] = ring.tile([P, PACK, W], F32, name="sq", tag=tag, bufs=bufs, align_bytes=64)
-            filt = [wq[f, b, a] for a in range(2)]
-            toks = [xq[hf, a] for a in range(2)]
-            for t in range(PACK):
-                acc = psum.tile([P, W], F32, name="acc", tag="acc", bufs=5)
-                if turned:
-                    product(acc, toks, t, filt)
+        def respond(f, b, hf, lo, width, tag, plain_tag=None, skip=()):
+            if tag.startswith("pickedall"):
+                if hf == 0:
+                    picked[tag] = slot([P, 2, PACK, W], F32, tag)
+                squares[f, b, hf, lo] = picked[tag][:, hf]
+            else:
+                squares[f, b, hf, lo] = slot([P, PACK, width], F32, tag)
+            per_bank = W // width
+            for first in range(0, PACK, per_bank):
+                acc = psum.tile([P, per_bank, width], F32, name="acc", tag="acc", bufs=4)
+                for t in range(first, first + per_bank):
+                    for a in range(2):
+                        nc.tensor.matmul_mx(
+                            acc[:, t - first, :],
+                            lhsT=wq[f, b, a][0][:, P * t : P * (t + 1)].bitcast(FP8X4),
+                            lhsT_scale=wq[f, b, a][1][:, P * t : P * (t + 1)],
+                            rhs=xq[hf, a][0][:, lo : lo + width].bitcast(FP8X4),
+                            rhs_scale=xq[hf, a][1][:, lo : lo + width],
+                            start=(a == 0),
+                            stop=(a == 1),
+                        )
+                dst = squares[f, b, hf, lo][:, first : first + per_bank, :]
+                if plain_tag is None or first in skip:
+                    nc.scalar.activation(dst, acc[:], ACT.Square)
                 else:
-                    product(acc, filt, t, toks)
-                if t in on_vector:
-                    plain = ring.tile([P, W], F32, name="plain", tag=ptag, bufs=pbufs, align_bytes=64)
+                    plain = slot([P, per_bank, width], F32, plain_tag)
                     nc.vector.tensor_copy(plain[:], acc[:])
-                    nc.vector.tensor_tensor(squares[f, b, hf][:, t, :], acc[:], plain[:], ALU.mult)
-                else:
-                    nc.scalar.activation(squares[f, b, hf][:, t, :], acc[:], ACT.Square)
+                    nc.vector.tensor_tensor(dst, acc[:], plain[:], ALU.mult)
 
-        def energy(b, hf, lo, step, tag, gtag="hgrp", gbufs=3):
-            if lo == 0:
-                hq[b, hf] = code_tiles("hq%d%d" % (b, hf))
-            if True:
-                grouped = ring.tile([P, PACK * step], BF16, name="hgrp", tag=gtag, bufs=gbufs, align_bytes=64)
-                total = ring.tile([P, PACK, step], F32, name="total", tag=tag, bufs=1, align_bytes=64)
-                part = total[:]
-                nc.vector.tensor_tensor(part, squares[0, b, hf][:, :, lo : lo + step], squares[1, b, hf][:, :, lo : lo + step], ALU.add)
-                nc.scalar.activation(
-                    grouped[:].rearrange("p (c j t) -> p c t j", j=4, t=PACK),
-                    part.rearrange("p t (c j) -> p c t j", j=4),
-                    ACT.Sqrt,
-                )
-                quantise(hq[b, hf], grouped, lo, lo + step, lo)
+        def energy(b, hf, lo, width, tag, gtag="hgrp", gbufs=3):
+            total = slot([P, PACK, width], F32, tag)
+            if (EVEN, b, hf, lo) in squares and squares[EVEN, b, hf, lo].shape[2] == width:
+                even, odd = squares[EVEN, b, hf, lo][:], squares[ODD, b, hf, lo][:]
+            else:
+                even, odd = (squares[f, b, hf, 0][:, :, lo : lo + width] for f in (EVEN, ODD))
+            nc.vector.tensor_tensor(total[:], even, odd, ALU.add)
+            grouped = slot([P, PACK * width], BF16, gtag, gbufs)
+            nc.scalar.activation(
+                grouped[:].rearrange("p (c j t) -> p c t j", j=4, t=PACK),
+                total[:].rearrange("p t (c j) -> p c t j", j=4),
+                ACT.Sqrt,
+            )
+            hq[b, hf, lo] = quantise(grouped, "hq%d%d%d" % (b, hf, lo))
 
-
-        def codes_out(hf, on_scalar, lo=0, hi=W):
-            for u in range(N // P):
-                acc = psum.tile([P, W], F32, name="fin", tag="fin", bufs=3)
-                for b in range(2):
-                    nc.tensor.matmul_mx(
-                        acc[:],
-                        lhsT=small["wd"][:, b, 2 * P * u : 2 * P * (u + 1)].bitcast(FP4X4),
-                        lhsT_scale=wd_plane[:, b, P * u : P * (u + 1)],
-                        rhs=hq[b, hf][0][:].bitcast(FP8X4),
-                        rhs_scale=hq[b, hf][1][:],
-                        start=(b == 0),
-                        stop=(b == 1),
-                    )
-                result = ring.tile([P, W], F32, name="result", tag="result", bufs=8, align_bytes=64)
-                if u in on_scalar:
-                    nc.scalar.activation(result[:], acc[:], ACT.Identity, bias=small["bias"][:, u : u + 1])
-                else:
-                    nc.vector.tensor_scalar_add(result[:], acc[:], small["bias"][:, u : u + 1])
-                nc.sync.dma_start(out[P * u : P * (u + 1), W * hf : W * (hf + 1)], result[:])
-
-        def codes_part(hf, lo, step):
-            for pair in range(2):
-                acc = psum.tile([P, 2, step], F32, name="fin", tag="fin", bufs=3)
-                passes = [(b, v, c) for b in range(2) for v in range(2) for c in range(0, step, P)]
+        def codes_out(hf, lo, width, on_scalar):
+            per_bank = 1 if width == W else 2
+            step = W if width == W else P
+            for first in range(0, N // P, per_bank):
+                acc = psum.tile([P, per_bank, width], F32, name="fin", tag="fin", bufs=4)
+                passes = [(b, v, c) for b in range(2) for v in range(per_bank) for c in range(0, width, step)]
                 for b, v, c in passes:
-                    u = 2 * pair + v
+                    u = first + v
+                    codes, scales = hq[b, hf, lo]
+                    at = c
                     nc.tensor.matmul_mx(
-                        acc[:, v, c : c + P],
+                        acc[:, v, c : c + step],
                         lhsT=small["wd"][:, b, 2 * P * u : 2 * P * (u + 1)].bitcast(FP4X4),
                         lhsT_scale=wd_plane[:, b, P * u : P * (u + 1)],
-                        rhs=hq[b, hf][0][:, lo + c : lo + c + P].bitcast(FP8X4),
-                        rhs_scale=hq[b, hf][1][:, lo + c : lo + c + P],
+                        rhs=codes[:, at : at + step].bitcast(FP8X4),
+                        rhs_scale=scales[:, at : at + step],
                         start=((b, v, c) == passes[0]),
                         stop=((b, v, c) == passes[-1]),
                     )
-                result = ring.tile([P, 2, step], F32, name="result", tag="result", bufs=8, align_bytes=64)
-                for v in range(2):
-                    u = 2 * pair + v
-                    if pair == 1:
-                        nc.scalar.activation(result[:, v, :], acc[:, v, :], ACT.Identity, bias=small["bias"][:, u : u + 1])
+                result = slot([P, per_bank, width], F32, "result", 6)
+                for v in range(per_bank):
+                    column = small["bias"][:, first + v : first + v + 1]
+                    if first in on_scalar:
+                        nc.scalar.activation(result[:, v, :], acc[:, v, :], ACT.Identity, bias=column)
                     else:
-                        nc.vector.tensor_scalar_add(result[:, v, :], acc[:, v, :], small["bias"][:, u : u + 1])
-                rows = out[2 * P * pair : 2 * P * (pair + 1), W * hf + lo : W * hf + lo + step]
+                        nc.vector.tensor_scalar_add(result[:, v, :], acc[:, v, :], column)
+                rows = out[P * first : P * (first + per_bank), W * hf + lo : W * hf + lo + width]
                 nc.sync.dma_start(rows.rearrange("(v p) j -> p v j", p=P), result[:])
 
+        on_scalar, on_vector = nc.scalar.copy, nc.vector.tensor_copy
         load_gain(0)
         load_plane(0, 0)
         load_gain(1)
-        load_plane(0, 1)
-        load_plane(0, 2)
-        load_plane(0, 3)
-        load_plane(1, 0)
-        load_plane(1, 1)
-        load_plane(1, 2)
-        load_filter(0, 0, 0, "first", 1)
+        for i in range(1, PACK):
+            load_plane(0, i)
+        for i in range(3):
+            load_plane(1, i)
+        load_filter(EVEN, 0, (0,), "first")
         load_plane(1, 3)
-        load_filter(0, 0, 1, "once", 1)
+        load_filter(EVEN, 1, (0,), "second")
         for i in range(PACK):
             gather(0, 0, i)
             gather(1, 0, i)
-        load_filter(1, 0, 0, "plane00", 1)
-        load_filter(1, 0, 1, "plane01", 1)
-        load_filter(0, 1, 0, "plane02", 1)
-        load_filter(0, 1, 1, "plane03", 1)
+        load_filter(ODD, 0, (0,), "plane00")
+        load_filter(ODD, 1, (0,), "plane01")
+        load_filter(EVEN, 0, (1,), "plane02")
+        load_filter(EVEN, 1, (1,), "plane03")
+        load_filter(ODD, 0, (1,), "fourth")
+        load_filter(ODD, 1, (1,), "third")
+        load_small()
         weave_x(0, 0, 0)
         weave_x(1, 0, 0)
         for i in range(3):
             gather(0, 1, i)
             gather(1, 1, i)
-        load_filter(1, 1, 0, "plane10", 1)
-        load_filter(1, 1, 1, "plane11", 1)
-        load_small()
         gather(0, 1, 3)
-        weave_w(0, 0, 0, 0)
-        weave_w(0, 0, 1, 0)
-        weave_x(0, 1, 128, "w1", 1)
+        weave_w(EVEN, 0, 0, on_scalar)
+        weave_w(EVEN, 0, 1, on_scalar, "w1", 1)
+        weave_x(0, 1, 128)
         gather(1, 1, 3)
-        weave_x(1, 1, 128, "once", 1)
-        weave_w(1, 0, 0, 0)
-        weave_w(1, 0, 1, 4)
-        weave_w(0, 1, 0, 4)
-        weave_w(0, 1, 1, 4)
-        weave_w(1, 1, 0, 4)
-        weave_w(1, 1, 1, 4, "first", 1)
-        respond(0, 0, 0)
-        respond(0, 0, 1)
-        respond(1, 0, 0)
-        respond(1, 0, 1)
-        respond(0, 1, 0)
-        respond(1, 1, 0, False, (), "result", 8, "plane00", 1)
+        weave_x(1, 1, 128, "w1", 1)
+        weave_w(ODD, 0, 0, on_scalar)
+        weave_w(ODD, 0, 1, on_vector, "w2", 1)
+        weave_w(EVEN, 1, 0, on_vector, "w2", 1)
+        weave_w(EVEN, 1, 1, on_vector)
+        weave_w(ODD, 1, 0, on_vector)
+        weave_w(ODD, 1, 1, on_vector, "first", 1)
+        respond(EVEN, 0, 0, 0, W, "picked00")
+        respond(EVEN, 0, 1, 0, W, "picked10")
+        respond(ODD, 0, 0, 0, W, "picked01")
+        respond(ODD, 0, 1, 0, W, "picked11")
+        respond(EVEN, 1, 0, 0, W, "plane10")
+        respond(ODD, 1, 0, 0, W, "plane11")
         energy(0, 0, 0, W, "first", "h0", 1)
-        energy(1, 0, 0, W, "plane10")
-        respond(0, 1, 1, False, (3,), "h0", 1)
-        respond(1, 1, 1, False, (), "h0", 1)
-        energy(0, 1, 0, W, "plane00")
-        energy(1, 1, 0, 256, "plane13")
-        energy(1, 1, 256, 128, "plane03")
-        energy(1, 1, 384, 128, "plane02")
-        codes_out(0, ())
-        codes_part(1, 0, 256)
-        codes_part(1, 256, 128)
-        codes_part(1, 384, 128)
+        energy(1, 0, 0, W, "plane01")
+        respond(EVEN, 1, 1, 0, 256, "plane12", "h0", (0,))
+        respond(ODD, 1, 1, 0, 256, "plane13")
+        energy(0, 1, 0, 256, "plane11")
+        energy(1, 1, 0, 256, "plane03")
+        codes_out(0, 0, W, ())
+        respond(EVEN, 1, 1, 256, 128, "second", None, ())
+        respond(ODD, 1, 1, 256, 128, "fourth")
+        energy(0, 1, 256, 128, "plane02")
+        energy(1, 1, 256, 128, "third")
+        respond(EVEN, 1, 1, 384, 128, "e3", None, ())
+        respond(ODD, 1, 1, 384, 128, "o3")
+        energy(0, 1, 384, 128, "t3")
+        energy(1, 1, 384, 128, "u3")
+        codes_out(1, 0, 256, (2,))
+        codes_out(1, 256, 128, (2,))
+        codes_out(1, 384, 128, (2,))

@@ -1,6 +1,7 @@
 from contextlib import ExitStack
 
 import concourse.mybir as mybir
+from concourse.masks import make_identity
 
 K, T, S, H, N = 1024, 2048, 1024, 1024, 512
 FLOPS = 2 * (2 * K * H * S + H * N * S)
@@ -33,18 +34,23 @@ def tile_list_deformable_texture_energy_kernel(tc, xT, wgt, offs, we, wo, wd_wor
         def slot(shape, dtype, tag, bufs=1):
             return keep.tile(shape, dtype, name=tag, tag=tag, bufs=bufs, align_bytes=64)
 
+        def bank(index, shape):
+            return psum.tile(shape, F32, name="bank%d" % index, tag="bank%d" % index, bufs=1)
+
         offsets = lists.tile([P, S // 16], U16, name="offsets")
         nc.sync.dma_start(offsets[:], offs)
 
         wd_plane = slot([P, 2, N], U8, "wd_plane")
         nc.gpsimd.memset(wd_plane[:].rearrange("p a n -> p (a n)").bitcast(I32), 0)
+        identity = slot([P, P], F32, "identity")
+        make_identity(nc, identity[:])
 
         warm = slot([P, 2], F32, "warm")
         nc.vector.memset(warm[:, 0:1], 1.0)
         nc.scalar.activation(warm[:, 1:2], warm[:, 0:1], ACT.Sqrt)
 
         planes, gains, raws, small = {}, {}, {}, {}
-        xq, wq, hq, picked, squares = {}, {}, {}, {}, {}
+        xq, wq, hq, picked, squares, woven = {}, {}, {}, {}, {}, {}
 
         def load_plane(a, i):
             planes[a, i] = slot([P, T], F32, "plane%d%d" % (a, i))
@@ -55,13 +61,10 @@ def tile_list_deformable_texture_energy_kernel(tc, xT, wgt, offs, we, wo, wd_wor
             gains[hf] = slot([P, W], F32, "gain%d" % hf)
             nc.sync.dma_start(gains[hf][:], wgt[:, W * hf : W * (hf + 1)])
 
-        def load_filter(f, a, blocks, tag):
-            lo, hi = W * blocks[0], W * (blocks[-1] + 1)
-            raw = slot([P, PACK, hi - lo], F32, tag)
-            rows = (we, wo)[f][KP * a : KP * (a + 1), lo:hi]
-            nc.sync.dma_start(raw[:], rows.rearrange("(p i) c -> p i c", i=PACK))
-            for b in blocks:
-                raws[f, b, a] = raw[:, :, W * b - lo : W * (b + 1) - lo]
+        def load_filter(f, b, a, tag):
+            raws[f, b, a] = slot([P, PACK, W], F32, tag)
+            rows = (we, wo)[f][KP * a : KP * (a + 1), W * b : W * (b + 1)]
+            nc.sync.dma_start(raws[f, b, a][:], rows.rearrange("(p i) c -> p i c", i=PACK))
 
         def load_small():
             small["wd"] = slot([P, 2, 2 * N], U8, "wd_codes")
@@ -79,23 +82,8 @@ def tile_list_deformable_texture_energy_kernel(tc, xT, wgt, offs, we, wo, wd_wor
             width = grouped.shape[1] // PACK
             codes = slot([P, width], U32, name + "c")
             scales = slot([P, width], U8, name + "s")
-            nc.vector.quantize_mx(out=codes[:].bitcast(FP8X4), scales=scales[:], in_=grouped[:])
+            nc.vector.quantize_mx(out=codes[:].bitcast(FP8X4), scales=scales[:], in_=grouped)
             return codes, scales
-
-        def load_gains():
-            gains["all"] = slot([P, S], F32, "gains")
-            nc.sync.dma_start(gains["all"][:, :W], wgt[:, :W])
-
-        def load_gains_rest():
-            nc.sync.dma_start(gains["all"][:, W:], wgt[:, W:])
-
-        def gather_span(a, i, lo, hi):
-            if (i, lo) == (0, 0):
-                picked[a] = slot([P, PACK, S], F32, "pickedall%d" % a)
-                for hf in range(2):
-                    picked[hf, a] = picked[a][:, :, W * hf : W * (hf + 1)]
-            cut = offsets[:, lo // 16 : hi // 16]
-            nc.vector.tensor_tensor(picked[a][:, i, lo:hi], planes[a, i][:].indirect(cut), gains["all"][:, lo:hi], ALU.mult)
 
         def gather(hf, a, i):
             if i == 0:
@@ -103,91 +91,121 @@ def tile_list_deformable_texture_energy_kernel(tc, xT, wgt, offs, we, wo, wd_wor
             cut = offsets[:, hf * W // 16 : (hf + 1) * W // 16]
             nc.vector.tensor_tensor(picked[hf, a][:, i, :], planes[a, i][:].indirect(cut), gains[hf][:], ALU.mult)
 
-        def weave_x(hf, a, share, tag="xgrp", bufs=2):
+        def weave(src, copy, tag, bufs):
             grouped = slot([P, PACK * W], BF16, tag, bufs)
-            dst = grouped[:].rearrange("p (c j i) -> p c i j", j=4, i=PACK)
-            src = picked[hf, a][:].rearrange("p i (c j) -> p c i j", j=4)
-            if share > 0:
-                nc.vector.tensor_copy(dst[:, :share], src[:, :share])
-            if share < P:
-                nc.scalar.copy(dst[:, share:], src[:, share:])
-            xq[hf, a] = quantise(grouped, "xq%d%d" % (hf, a))
+            copy(
+                grouped[:].rearrange("p (c j i) -> p c i j", j=4, i=PACK),
+                src[:].rearrange("p i (c j) -> p c i j", j=4),
+            )
+            return grouped
 
-        def weave_w(f, b, a, copy, tag="wgrp", bufs=2):
+        def weave_dealt(src, copy, tag, bufs):
             grouped = slot([P, PACK * W], BF16, tag, bufs)
             copy(
                 grouped[:].rearrange("p (t m i) -> p m i t", t=PACK, i=PACK),
-                raws[f, b, a].rearrange("p i (m t) -> p m i t", t=PACK),
+                src[:].rearrange("p i (m t) -> p m i t", t=PACK),
             )
-            wq[f, b, a] = quantise(grouped, "wq%d%d%d" % (f, b, a))
+            return grouped
 
-        def respond(f, b, hf, lo, width, tag, plain_tag=None, skip=()):
-            if tag.startswith("pickedall"):
-                if hf == 0:
-                    picked[tag] = slot([P, 2, PACK, W], F32, tag)
-                squares[f, b, hf, lo] = picked[tag][:, hf]
-            else:
-                squares[f, b, hf, lo] = slot([P, PACK, width], F32, tag)
+        def make_x(hf, a, copy, tag="xgrp", bufs=2):
+            xq[hf, a] = quantise(weave(picked[hf, a], copy, tag, bufs)[:], "xq%d%d" % (hf, a))
+
+        def make_w(f, b, a, copy, tag="wgrp", bufs=3):
+            how = weave if b == 0 else weave_dealt
+            wq[f, b, a] = quantise(how(raws[f, b, a], copy, tag, bufs)[:], "wq%d%d%d" % (f, b, a))
+
+        def mx_pass(acc, stationary, at, moving, lo, width, a):
+            nc.tensor.matmul_mx(
+                acc,
+                lhsT=stationary[0][:, at : at + P].bitcast(FP8X4),
+                lhsT_scale=stationary[1][:, at : at + P],
+                rhs=moving[0][:, lo : lo + width].bitcast(FP8X4),
+                rhs_scale=moving[1][:, lo : lo + width],
+                start=(a == 0),
+                stop=(a == 1),
+            )
+
+        def respond_by_query(f, hf, tag):
+            squares[f, 0, hf] = slot([P, PACK, W], F32, tag)
+            for u in range(PACK):
+                acc = bank(PACK * hf + u, [P, W])
+                for a in range(2):
+                    mx_pass(acc[:], xq[hf, a], P * u, wq[f, 0, a], 0, W, a)
+                nc.scalar.activation(
+                    squares[f, 0, hf][:, u, :].rearrange("p (t m) -> p t m", t=PACK),
+                    acc[:].rearrange("p (m t) -> p t m", t=PACK),
+                    ACT.Square,
+                )
+
+        def energy_by_query(hf):
+            grouped = slot([P, PACK * W], BF16, "h0%d" % hf)
+            for u in range(PACK):
+                total = bank(PACK * hf + u, [P, PACK, P])
+                for t in range(PACK):
+                    for f in (EVEN, ODD):
+                        nc.tensor.matmul(
+                            total[:, t, :],
+                            lhsT=squares[f, 0, hf][:, u, P * t : P * (t + 1)],
+                            rhs=identity[:],
+                            start=(f == EVEN),
+                            stop=(f == ODD),
+                            is_transpose=True,
+                        )
+                nc.scalar.activation(
+                    grouped[:, W * u : W * (u + 1)].rearrange("p (j t) -> p j t", t=PACK),
+                    total[:].rearrange("p t j -> p j t"),
+                    ACT.Sqrt,
+                )
+            woven[0, hf] = grouped
+
+        def respond_by_filter(f, hf, lo, width, banks, on_vector=()):
             per_bank = W // width
-            for first in range(0, PACK, per_bank):
-                acc = psum.tile([P, per_bank, width], F32, name="acc", tag="acc", bufs=4)
+            for n, first in enumerate(range(0, PACK, per_bank)):
+                acc = bank(banks[n], [P, per_bank, width])
                 for t in range(first, first + per_bank):
                     for a in range(2):
-                        nc.tensor.matmul_mx(
-                            acc[:, t - first, :],
-                            lhsT=wq[f, b, a][0][:, P * t : P * (t + 1)].bitcast(FP8X4),
-                            lhsT_scale=wq[f, b, a][1][:, P * t : P * (t + 1)],
-                            rhs=xq[hf, a][0][:, lo : lo + width].bitcast(FP8X4),
-                            rhs_scale=xq[hf, a][1][:, lo : lo + width],
-                            start=(a == 0),
-                            stop=(a == 1),
-                        )
-                dst = squares[f, b, hf, lo][:, first : first + per_bank, :]
-                if plain_tag is None or first in skip:
-                    nc.scalar.activation(dst, acc[:], ACT.Square)
-                else:
-                    plain = slot([P, per_bank, width], F32, plain_tag)
+                        mx_pass(acc[:, t - first, :], wq[f, 1, a], P * t, xq[hf, a], lo, width, a)
+                dst = squares[f, 1, hf][:, first : first + per_bank, lo : lo + width]
+                if n in on_vector:
+                    plain = slot([P, per_bank, width], F32, "plain", 2)
                     nc.vector.tensor_copy(plain[:], acc[:])
                     nc.vector.tensor_tensor(dst, acc[:], plain[:], ALU.mult)
+                else:
+                    nc.scalar.activation(dst, acc[:], ACT.Square)
 
-        def energy(b, hf, lo, width, tag, gtag="hgrp", gbufs=3):
+        def energy_by_filter(hf, lo, width, tag):
             total = slot([P, PACK, width], F32, tag)
-            if (EVEN, b, hf, lo) in squares and squares[EVEN, b, hf, lo].shape[2] == width:
-                even, odd = squares[EVEN, b, hf, lo][:], squares[ODD, b, hf, lo][:]
-            else:
-                even, odd = (squares[f, b, hf, 0][:, :, lo : lo + width] for f in (EVEN, ODD))
+            even, odd = (squares[f, 1, hf][:, :, lo : lo + width] for f in (EVEN, ODD))
             nc.vector.tensor_tensor(total[:], even, odd, ALU.add)
-            grouped = slot([P, PACK * width], BF16, gtag, gbufs)
+            grouped = slot([P, PACK * width], BF16, "h1%d%d" % (hf, lo))
             nc.scalar.activation(
                 grouped[:].rearrange("p (c j t) -> p c t j", j=4, t=PACK),
                 total[:].rearrange("p t (c j) -> p c t j", j=4),
                 ACT.Sqrt,
             )
-            hq[b, hf, lo] = quantise(grouped, "hq%d%d%d" % (b, hf, lo))
+            hq[1, hf, lo] = quantise(grouped[:], "hq1%d%d" % (hf, lo))
 
-        def codes_out(hf, lo, width, on_scalar):
-            per_bank = 1 if width == W else 2
-            step = W if width == W else P
-            for first in range(0, N // P, per_bank):
-                acc = psum.tile([P, per_bank, width], F32, name="fin", tag="fin", bufs=4)
-                passes = [(b, v, c) for b in range(2) for v in range(per_bank) for c in range(0, width, step)]
-                for b, v, c in passes:
+        def codes_out(hf, lo, width, banks, on_scalar):
+            per_bank = N // P // len(banks)
+            for n, first in enumerate(range(0, N // P, per_bank)):
+                acc = bank(banks[n], [P, per_bank, width])
+                for v in range(per_bank):
                     u = first + v
-                    codes, scales = hq[b, hf, lo]
-                    at = c
-                    nc.tensor.matmul_mx(
-                        acc[:, v, c : c + step],
-                        lhsT=small["wd"][:, b, 2 * P * u : 2 * P * (u + 1)].bitcast(FP4X4),
-                        lhsT_scale=wd_plane[:, b, P * u : P * (u + 1)],
-                        rhs=codes[:, at : at + step].bitcast(FP8X4),
-                        rhs_scale=scales[:, at : at + step],
-                        start=((b, v, c) == passes[0]),
-                        stop=((b, v, c) == passes[-1]),
-                    )
+                    for b, at in ((0, lo), (1, 0)):
+                        codes, scales = hq[b, hf, lo - at]
+                        nc.tensor.matmul_mx(
+                            acc[:, v, :],
+                            lhsT=small["wd"][:, b, 2 * P * u : 2 * P * (u + 1)].bitcast(FP4X4),
+                            lhsT_scale=wd_plane[:, b, P * u : P * (u + 1)],
+                            rhs=codes[:, at : at + width].bitcast(FP8X4),
+                            rhs_scale=scales[:, at : at + width],
+                            start=(b == 0),
+                            stop=(b == 1),
+                        )
                 result = slot([P, per_bank, width], F32, "result", 6)
                 for v in range(per_bank):
                     column = small["bias"][:, first + v : first + v + 1]
-                    if first in on_scalar:
+                    if n in on_scalar:
                         nc.scalar.activation(result[:, v, :], acc[:, v, :], ACT.Identity, bias=column)
                     else:
                         nc.vector.tensor_scalar_add(result[:, v, :], acc[:, v, :], column)
@@ -202,57 +220,63 @@ def tile_list_deformable_texture_energy_kernel(tc, xT, wgt, offs, we, wo, wd_wor
             load_plane(0, i)
         for i in range(3):
             load_plane(1, i)
-        load_filter(EVEN, 0, (0,), "first")
+        load_filter(EVEN, 0, 0, "first")
         load_plane(1, 3)
-        load_filter(EVEN, 1, (0,), "second")
+        load_filter(EVEN, 0, 1, "second")
         for i in range(PACK):
             gather(0, 0, i)
             gather(1, 0, i)
-        load_filter(ODD, 0, (0,), "plane00")
-        load_filter(ODD, 1, (0,), "plane01")
-        load_filter(EVEN, 0, (1,), "plane02")
-        load_filter(EVEN, 1, (1,), "plane03")
-        load_filter(ODD, 0, (1,), "fourth")
-        load_filter(ODD, 1, (1,), "third")
-        load_small()
-        weave_x(0, 0, 0)
-        weave_x(1, 0, 0)
+        load_filter(ODD, 0, 0, "plane00")
+        load_filter(ODD, 0, 1, "plane01")
+        load_filter(EVEN, 1, 0, "plane02")
+        load_filter(EVEN, 1, 1, "plane03")
+        make_x(0, 0, on_scalar)
+        make_x(1, 0, on_scalar)
         for i in range(3):
             gather(0, 1, i)
             gather(1, 1, i)
+        load_filter(ODD, 1, 0, "plane10")
+        load_filter(ODD, 1, 1, "plane11")
+        load_small()
+        make_w(EVEN, 0, 0, on_scalar)
         gather(0, 1, 3)
-        weave_w(EVEN, 0, 0, on_scalar)
-        weave_w(EVEN, 0, 1, on_scalar, "w1", 1)
-        weave_x(0, 1, 128)
+        make_x(0, 1, on_scalar)
         gather(1, 1, 3)
-        weave_x(1, 1, 128, "w1", 1)
-        weave_w(ODD, 0, 0, on_scalar)
-        weave_w(ODD, 0, 1, on_vector, "w2", 1)
-        weave_w(EVEN, 1, 0, on_vector, "w2", 1)
-        weave_w(EVEN, 1, 1, on_vector)
-        weave_w(ODD, 1, 0, on_vector)
-        weave_w(ODD, 1, 1, on_vector, "first", 1)
-        respond(EVEN, 0, 0, 0, W, "picked00")
-        respond(EVEN, 0, 1, 0, W, "picked10")
-        respond(ODD, 0, 0, 0, W, "picked01")
-        respond(ODD, 0, 1, 0, W, "picked11")
-        respond(EVEN, 1, 0, 0, W, "plane10")
-        respond(ODD, 1, 0, 0, W, "plane11")
-        energy(0, 0, 0, W, "first", "h0", 1)
-        energy(1, 0, 0, W, "plane01")
-        respond(EVEN, 1, 1, 0, 256, "plane12", "h0", (0,))
-        respond(ODD, 1, 1, 0, 256, "plane13")
-        energy(0, 1, 0, 256, "plane11")
-        energy(1, 1, 0, 256, "plane03")
-        codes_out(0, 0, W, ())
-        respond(EVEN, 1, 1, 256, 128, "second", None, ())
-        respond(ODD, 1, 1, 256, 128, "fourth")
-        energy(0, 1, 256, 128, "plane02")
-        energy(1, 1, 256, 128, "third")
-        respond(EVEN, 1, 1, 384, 128, "e3", None, ())
-        respond(ODD, 1, 1, 384, 128, "o3")
-        energy(0, 1, 384, 128, "t3")
-        energy(1, 1, 384, 128, "u3")
-        codes_out(1, 0, 256, (2,))
-        codes_out(1, 256, 128, (2,))
-        codes_out(1, 384, 128, (2,))
+        make_w(EVEN, 0, 1, on_vector)
+        make_x(1, 1, on_scalar)
+        make_w(ODD, 0, 0, on_vector)
+        make_w(ODD, 0, 1, on_vector)
+        make_w(EVEN, 1, 0, on_vector)
+        make_w(EVEN, 1, 1, on_vector)
+        make_w(ODD, 1, 0, on_vector)
+        make_w(ODD, 1, 1, on_vector)
+        respond_by_query(EVEN, 0, "picked00")
+        respond_by_query(EVEN, 1, "picked10")
+        respond_by_query(ODD, 0, "first")
+        respond_by_query(ODD, 1, "plane12")
+        for hf in range(2):
+            energy_by_query(hf)
+        for hf in range(2):
+            hq[0, hf, 0] = quantise(woven[0, hf][:], "hq0%d" % hf)
+        for f, hf, tag in ((EVEN, 0, "plane13"), (EVEN, 1, "picked01"), (ODD, 0, "picked11"), (ODD, 1, "second")):
+            squares[f, 1, hf] = slot([P, PACK, W], F32, tag)
+        respond_by_filter(EVEN, 0, 0, 256, (0, 1))
+        respond_by_filter(EVEN, 0, 256, 256, (2, 3), (1,))
+        respond_by_filter(ODD, 0, 0, 256, (4, 5))
+        respond_by_filter(ODD, 0, 256, 256, (6, 7))
+        energy_by_filter(0, 0, 256, "plane00")
+        respond_by_filter(EVEN, 1, 0, 256, (0, 1))
+        respond_by_filter(ODD, 1, 0, 256, (2, 3))
+        energy_by_filter(0, 256, 256, "plane01")
+        codes_out(0, 0, 256, (4, 5), ())
+        respond_by_filter(EVEN, 1, 256, 128, (6,))
+        respond_by_filter(ODD, 1, 256, 128, (7,))
+        energy_by_filter(1, 0, 256, "plane02")
+        codes_out(0, 256, 256, (0, 1), ())
+        respond_by_filter(EVEN, 1, 384, 128, (2,))
+        respond_by_filter(ODD, 1, 384, 128, (3,))
+        energy_by_filter(1, 256, 128, "plane03")
+        codes_out(1, 0, 256, (4, 5), ())
+        energy_by_filter(1, 384, 128, "plane10")
+        codes_out(1, 256, 128, (6, 7), (1,))
+        codes_out(1, 384, 128, (0, 1), (1,))

@@ -34,7 +34,11 @@ def tile_list_deformable_texture_energy_kernel(tc, xT, wgt, offs, we, wo, wd_wor
         def slot(shape, dtype, tag, bufs=1):
             return keep.tile(shape, dtype, name=tag, tag=tag, bufs=bufs, align_bytes=64)
 
-        def bank(index, shape):
+        taken = []
+
+        def bank(shape):
+            index = len(taken) % 8
+            taken.append(index)
             return psum.tile(shape, F32, name="bank%d" % index, tag="bank%d" % index, bufs=1)
 
         offsets = lists.tile([P, S // 16], U16, name="offsets")
@@ -49,8 +53,8 @@ def tile_list_deformable_texture_energy_kernel(tc, xT, wgt, offs, we, wo, wd_wor
         nc.vector.memset(warm[:, 0:1], 1.0)
         nc.scalar.activation(warm[:, 1:2], warm[:, 0:1], ACT.Sqrt)
 
-        planes, gains, raws, small = {}, {}, {}, {}
-        xq, wq, hq, picked, squares, woven = {}, {}, {}, {}, {}, {}
+        planes, gains, raws, small, spans = {}, {}, {}, {}, {}
+        xq, wq, hq, picked, squares, woven, totals, sums, results = {}, {}, {}, {}, {}, {}, {}, {}, {}
 
         def load_plane(a, i):
             planes[a, i] = slot([P, T], F32, "plane%d%d" % (a, i))
@@ -85,132 +89,162 @@ def tile_list_deformable_texture_energy_kernel(tc, xT, wgt, offs, we, wo, wd_wor
             nc.vector.quantize_mx(out=codes[:].bitcast(FP8X4), scales=scales[:], in_=grouped)
             return codes, scales
 
-        def gather(hf, a, i):
-            if i == 0:
+        def gather(hf, a, i, lo=0, width=W):
+            if (i, lo) == (0, 0):
                 picked[hf, a] = slot([P, PACK, W], F32, "picked%d%d" % (hf, a))
-            cut = offsets[:, hf * W // 16 : (hf + 1) * W // 16]
-            nc.vector.tensor_tensor(picked[hf, a][:, i, :], planes[a, i][:].indirect(cut), gains[hf][:], ALU.mult)
-
-        def weave(src, copy, tag, bufs):
-            grouped = slot([P, PACK * W], BF16, tag, bufs)
-            copy(
-                grouped[:].rearrange("p (c j i) -> p c i j", j=4, i=PACK),
-                src[:].rearrange("p i (c j) -> p c i j", j=4),
+            cut = offsets[:, (hf * W + lo) // 16 : (hf * W + lo + width) // 16]
+            nc.vector.tensor_tensor(
+                picked[hf, a][:, i, lo : lo + width], planes[a, i][:].indirect(cut), gains[hf][:, lo : lo + width], ALU.mult
             )
-            return grouped
 
-        def weave_dealt(src, copy, tag, bufs):
-            grouped = slot([P, PACK * W], BF16, tag, bufs)
+        def weave_x(hf, a, copy, lo=0, width=W, tag="xgrp", bufs=2):
+            if lo == 0:
+                woven["x", hf, a] = slot([P, PACK * W], BF16, tag, bufs)
             copy(
-                grouped[:].rearrange("p (t m i) -> p m i t", t=PACK, i=PACK),
-                src[:].rearrange("p i (m t) -> p m i t", t=PACK),
+                woven["x", hf, a][:, PACK * lo : PACK * (lo + width)].rearrange("p (c j i) -> p c i j", j=4, i=PACK),
+                picked[hf, a][:, :, lo : lo + width].rearrange("p i (c j) -> p c i j", j=4),
             )
-            return grouped
 
-        def make_x(hf, a, copy, tag="xgrp", bufs=2):
-            xq[hf, a] = quantise(weave(picked[hf, a], copy, tag, bufs)[:], "xq%d%d" % (hf, a))
+        def quant_x(hf, a):
+            xq[hf, a] = quantise(woven["x", hf, a][:], "xq%d%d" % (hf, a))
 
-        def make_w(f, b, a, copy, tag="wgrp", bufs=3):
-            how = weave if b == 0 else weave_dealt
-            wq[f, b, a] = quantise(how(raws[f, b, a], copy, tag, bufs)[:], "wq%d%d%d" % (f, b, a))
+        def weave_w(f, b, a, copy, tag="wgrp", bufs=3, lo=0, hi=P):
+            if lo == 0:
+                woven["w", f, b, a] = slot([P, PACK * W], BF16, tag, bufs)
+            copy(
+                woven["w", f, b, a][:].rearrange("p (t m i) -> p m i t", t=PACK, i=PACK)[:, lo:hi],
+                raws[f, b, a][:].rearrange("p i (m t) -> p m i t", t=PACK)[:, lo:hi],
+            )
 
-        def mx_pass(acc, stationary, at, moving, lo, width, a):
+        def quant_w(f, b, a):
+            wq[f, b, a] = quantise(woven["w", f, b, a][:], "wq%d%d%d" % (f, b, a))
+
+        def mx_pass(acc, stationary, at, moving, lo, width, start, stop):
             nc.tensor.matmul_mx(
                 acc,
                 lhsT=stationary[0][:, at : at + P].bitcast(FP8X4),
                 lhsT_scale=stationary[1][:, at : at + P],
                 rhs=moving[0][:, lo : lo + width].bitcast(FP8X4),
                 rhs_scale=moving[1][:, lo : lo + width],
-                start=(a == 0),
-                stop=(a == 1),
+                start=start,
+                stop=stop,
             )
 
-        def respond_by_query(f, hf, tag):
-            squares[f, 0, hf] = slot([P, PACK, W], F32, tag)
-            for u in range(PACK):
-                acc = bank(PACK * hf + u, [P, W])
-                for a in range(2):
-                    mx_pass(acc[:], xq[hf, a], P * u, wq[f, 0, a], 0, W, a)
-                nc.scalar.activation(
-                    squares[f, 0, hf][:, u, :].rearrange("p (t m) -> p t m", t=PACK),
-                    acc[:].rearrange("p (m t) -> p t m", t=PACK),
-                    ACT.Square,
-                )
+        def room(f, b, lo, width):
+            return squares[f, b, lo // W][:, PACK * (lo % W) : PACK * (lo % W + width)]
 
-        def energy_by_query(hf):
-            grouped = slot([P, PACK * W], BF16, "h0%d" % hf)
-            for u in range(PACK):
-                total = bank(PACK * hf + u, [P, PACK, P])
+        def by_query(f, b, lo, width, passes=(0, 1)):
+            for at in range(lo, lo + width, P):
+                for a in passes:
+                    if a == 0:
+                        sums[f, b, at] = bank([P, W])
+                    mx_pass(sums[f, b, at][:], xq[at // W, a], at % W, wq[f, b, a], 0, W, a == 0, a == 1)
+
+        def by_filter(f, b, lo, width, passes=(0, 1)):
+            per_bank = W // width
+            for at in range(lo, lo + width, P):
+                spans[b, at] = (lo, width)
+            for n in range(PACK // per_bank):
+                for a in passes:
+                    if a == 0:
+                        sums[f, b, lo + P * n] = bank([P, W])
+                    for v in range(per_bank):
+                        mx_pass(
+                            sums[f, b, lo + P * n][:, width * v : width * (v + 1)],
+                            wq[f, b, a], P * (per_bank * n + v), xq[lo // W, a], lo % W, width,
+                            (a, v) == (0, 0), (a, v) == (1, per_bank - 1),
+                        )
+
+        def square(f, b, lo, width):
+            for at in range(lo, lo + width, P):
+                nc.scalar.activation(room(f, b, at, P), sums[f, b, at][:], ACT.Square)
+
+        def square_on_vector(f, b, lo, width):
+            plain = {}
+            for at in range(lo, lo + width, P):
+                plain[at] = slot([P, W], F32, "plain", 2)
+                nc.vector.tensor_copy(plain[at][:], sums[f, b, at][:])
+            for at in range(lo, lo + width, P):
+                nc.vector.tensor_tensor(room(f, b, at, P), sums[f, b, at][:], plain[at][:], ALU.mult)
+
+        def turn_and_add(b, lo, width):
+            for n in range(width // P):
+                totals[b, lo + P * n] = bank([P, PACK, P])
                 for t in range(PACK):
                     for f in (EVEN, ODD):
                         nc.tensor.matmul(
-                            total[:, t, :],
-                            lhsT=squares[f, 0, hf][:, u, P * t : P * (t + 1)],
+                            totals[b, lo + P * n][:, t, :],
+                            lhsT=room(f, b, lo + P * n, P)[:, P * t : P * (t + 1)],
                             rhs=identity[:],
                             start=(f == EVEN),
                             stop=(f == ODD),
                             is_transpose=True,
                         )
+
+        def root_of_bank(b, lo, width):
+            woven[b, lo] = slot([P, PACK * width], BF16, "h%d%d" % (b, lo))
+            for n in range(width // P):
                 nc.scalar.activation(
-                    grouped[:, W * u : W * (u + 1)].rearrange("p (j t) -> p j t", t=PACK),
-                    total[:].rearrange("p t j -> p j t"),
+                    woven[b, lo][:, W * n : W * (n + 1)].rearrange("p (j t) -> p j t", t=PACK),
+                    totals[b, lo + P * n][:].rearrange("p t j -> p j t"),
                     ACT.Sqrt,
                 )
-            woven[0, hf] = grouped
 
-        def respond_by_filter(f, hf, lo, width, banks, on_vector=()):
-            per_bank = W // width
-            for n, first in enumerate(range(0, PACK, per_bank)):
-                acc = bank(banks[n], [P, per_bank, width])
-                for t in range(first, first + per_bank):
-                    for a in range(2):
-                        mx_pass(acc[:, t - first, :], wq[f, 1, a], P * t, xq[hf, a], lo, width, a)
-                dst = squares[f, 1, hf][:, first : first + per_bank, lo : lo + width]
-                if n in on_vector:
-                    plain = slot([P, per_bank, width], F32, "plain", 2)
-                    nc.vector.tensor_copy(plain[:], acc[:])
-                    nc.vector.tensor_tensor(dst, acc[:], plain[:], ALU.mult)
-                else:
-                    nc.scalar.activation(dst, acc[:], ACT.Square)
+        def add_squares(b, lo, width, tag, engine=nc.vector):
+            totals[b, lo] = slot([P, PACK * width], F32, tag)
+            start, span = spans[b, lo]
+            even, odd = (
+                room(f, b, start, span).rearrange("p (t j) -> p t j", t=PACK)[:, :, lo - start : lo - start + width]
+                for f in (EVEN, ODD)
+            )
+            engine.tensor_tensor(totals[b, lo][:].rearrange("p (t j) -> p t j", t=PACK), even, odd, ALU.add)
 
-        def energy_by_filter(hf, lo, width, tag):
-            total = slot([P, PACK, width], F32, tag)
-            even, odd = (squares[f, 1, hf][:, :, lo : lo + width] for f in (EVEN, ODD))
-            nc.vector.tensor_tensor(total[:], even, odd, ALU.add)
-            grouped = slot([P, PACK * width], BF16, "h1%d%d" % (hf, lo))
+        def root(b, lo, width):
+            woven[b, lo] = slot([P, PACK * width], BF16, "h%d%d" % (b, lo))
             nc.scalar.activation(
-                grouped[:].rearrange("p (c j t) -> p c t j", j=4, t=PACK),
-                total[:].rearrange("p t (c j) -> p c t j", j=4),
+                woven[b, lo][:].rearrange("p (c j t) -> p c t j", j=4, t=PACK),
+                totals[b, lo][:].rearrange("p (t c j) -> p c t j", j=4, t=PACK),
                 ACT.Sqrt,
             )
-            hq[1, hf, lo] = quantise(grouped[:], "hq1%d%d" % (hf, lo))
 
-        def codes_out(hf, lo, width, banks, on_scalar):
-            per_bank = N // P // len(banks)
-            for n, first in enumerate(range(0, N // P, per_bank)):
-                acc = bank(banks[n], [P, per_bank, width])
-                for v in range(per_bank):
-                    u = first + v
-                    for b, at in ((0, lo), (1, 0)):
-                        codes, scales = hq[b, hf, lo - at]
+        def quant_h(b, lo):
+            codes, scales = quantise(woven[b, lo][:], "hq%d%d" % (b, lo))
+            for at in range(0, codes.shape[1], P):
+                hq[b, lo + at] = (codes, scales, at)
+
+        def project(lo, width, blocks=(0, 1)):
+            per_bank = 2
+            for n in range(N // P // per_bank):
+                for b in blocks:
+                    if b == 0:
+                        sums["out", lo, n] = bank([P, per_bank, width])
+                    codes, scales, at = hq[b, lo]
+                    for v in range(per_bank):
+                        u = per_bank * n + v
                         nc.tensor.matmul_mx(
-                            acc[:, v, :],
+                            sums["out", lo, n][:, v, :],
                             lhsT=small["wd"][:, b, 2 * P * u : 2 * P * (u + 1)].bitcast(FP4X4),
                             lhsT_scale=wd_plane[:, b, P * u : P * (u + 1)],
                             rhs=codes[:, at : at + width].bitcast(FP8X4),
                             rhs_scale=scales[:, at : at + width],
-                            start=(b == 0),
-                            stop=(b == 1),
+                            start=((b, v) == (0, 0)),
+                            stop=((b, v) == (1, per_bank - 1)),
                         )
-                result = slot([P, per_bank, width], F32, "result", 6)
+
+        def store(lo, n, on_scalar=False):
+            acc = sums["out", lo, n]
+            per_bank, width = acc.shape[1], acc.shape[2]
+            first = per_bank * n
+            result = slot([P, per_bank, width], F32, "result", 10)
+            if on_scalar:
                 for v in range(per_bank):
                     column = small["bias"][:, first + v : first + v + 1]
-                    if n in on_scalar:
-                        nc.scalar.activation(result[:, v, :], acc[:, v, :], ACT.Identity, bias=column)
-                    else:
-                        nc.vector.tensor_scalar_add(result[:, v, :], acc[:, v, :], column)
-                rows = out[P * first : P * (first + per_bank), W * hf + lo : W * hf + lo + width]
-                nc.sync.dma_start(rows.rearrange("(v p) j -> p v j", p=P), result[:])
+                    nc.scalar.activation(result[:, v, :], acc[:, v, :], ACT.Identity, bias=column)
+            else:
+                columns = small["bias"][:, first : first + per_bank].unsqueeze(2)
+                nc.vector.tensor_tensor(result[:], acc[:], columns.to_broadcast([P, per_bank, width]), ALU.add)
+            rows = out[P * first : P * (first + per_bank), lo : lo + width]
+            nc.sync.dma_start(rows.rearrange("(v p) j -> p v j", p=P), result[:])
 
         on_scalar, on_vector = nc.scalar.copy, nc.vector.tensor_copy
         load_gain(0)
@@ -230,53 +264,114 @@ def tile_list_deformable_texture_energy_kernel(tc, xT, wgt, offs, we, wo, wd_wor
         load_filter(ODD, 0, 1, "plane01")
         load_filter(EVEN, 1, 0, "plane02")
         load_filter(EVEN, 1, 1, "plane03")
-        make_x(0, 0, on_scalar)
-        make_x(1, 0, on_scalar)
-        for i in range(3):
-            gather(0, 1, i)
-            gather(1, 1, i)
+        weave_x(0, 0, on_scalar)
+        weave_x(1, 0, on_scalar)
+        gather(0, 1, 0)
+        gather(1, 1, 0)
+        quant_x(0, 0)
+        gather(0, 1, 1)
+        gather(1, 1, 1)
+        quant_x(1, 0)
+        gather(0, 1, 2)
+        gather(1, 1, 2)
         load_filter(ODD, 1, 0, "plane10")
         load_filter(ODD, 1, 1, "plane11")
         load_small()
-        make_w(EVEN, 0, 0, on_scalar)
-        gather(0, 1, 3)
-        make_x(0, 1, on_scalar)
+        weave_w(EVEN, 0, 0, on_scalar)
+        gather(0, 1, 3, 0, 256)
+        gather(0, 1, 3, 256, 256)
+        weave_x(0, 1, on_scalar, 0, 256)
+        weave_x(0, 1, on_scalar, 256, 256)
+        quant_w(EVEN, 0, 0)
         gather(1, 1, 3)
-        make_w(EVEN, 0, 1, on_vector)
-        make_x(1, 1, on_scalar)
-        make_w(ODD, 0, 0, on_vector)
-        make_w(ODD, 0, 1, on_vector)
-        make_w(EVEN, 1, 0, on_vector)
-        make_w(EVEN, 1, 1, on_vector)
-        make_w(ODD, 1, 0, on_vector)
-        make_w(ODD, 1, 1, on_vector)
-        respond_by_query(EVEN, 0, "picked00")
-        respond_by_query(EVEN, 1, "picked10")
-        respond_by_query(ODD, 0, "first")
-        respond_by_query(ODD, 1, "plane12")
-        for hf in range(2):
-            energy_by_query(hf)
-        for hf in range(2):
-            hq[0, hf, 0] = quantise(woven[0, hf][:], "hq0%d" % hf)
+        weave_w(EVEN, 0, 1, on_vector)
+        weave_x(1, 1, on_scalar)
+        quant_x(0, 1)
+        quant_w(EVEN, 0, 1)
+        weave_w(ODD, 0, 0, on_vector)
+        quant_x(1, 1)
+        quant_w(ODD, 0, 0)
+        weave_w(ODD, 0, 1, on_vector)
+        quant_w(ODD, 0, 1)
+        for f, hf, tag in ((EVEN, 0, "picked00"), (EVEN, 1, "picked10"), (ODD, 0, "first"), (ODD, 1, "plane12")):
+            squares[f, 0, hf] = slot([P, PACK * W], F32, tag)
         for f, hf, tag in ((EVEN, 0, "plane13"), (EVEN, 1, "picked01"), (ODD, 0, "picked11"), (ODD, 1, "second")):
-            squares[f, 1, hf] = slot([P, PACK, W], F32, tag)
-        respond_by_filter(EVEN, 0, 0, 256, (0, 1))
-        respond_by_filter(EVEN, 0, 256, 256, (2, 3), (1,))
-        respond_by_filter(ODD, 0, 0, 256, (4, 5))
-        respond_by_filter(ODD, 0, 256, 256, (6, 7))
-        energy_by_filter(0, 0, 256, "plane00")
-        respond_by_filter(EVEN, 1, 0, 256, (0, 1))
-        respond_by_filter(ODD, 1, 0, 256, (2, 3))
-        energy_by_filter(0, 256, 256, "plane01")
-        codes_out(0, 0, 256, (4, 5), ())
-        respond_by_filter(EVEN, 1, 256, 128, (6,))
-        respond_by_filter(ODD, 1, 256, 128, (7,))
-        energy_by_filter(1, 0, 256, "plane02")
-        codes_out(0, 256, 256, (0, 1), ())
-        respond_by_filter(EVEN, 1, 384, 128, (2,))
-        respond_by_filter(ODD, 1, 384, 128, (3,))
-        energy_by_filter(1, 256, 128, "plane03")
-        codes_out(1, 0, 256, (4, 5), ())
-        energy_by_filter(1, 384, 128, "plane10")
-        codes_out(1, 256, 128, (6, 7), (1,))
-        codes_out(1, 384, 128, (0, 1), (1,))
+            squares[f, 1, hf] = slot([P, PACK * W], F32, tag)
+        for passes in ((0,), (1,)):
+            by_filter(EVEN, 0, 0, 256, passes)
+            by_query(EVEN, 0, 256, 768, passes)
+        square(EVEN, 0, 0, 1024)
+        by_filter(ODD, 0, 0, 256, (0,))
+        by_query(ODD, 0, 256, 256, (0,))
+        by_filter(ODD, 0, 0, 256, (1,))
+        by_query(ODD, 0, 256, 256, (1,))
+        by_query(ODD, 0, 512, 512)
+        square(ODD, 0, 0, 1024)
+        weave_w(EVEN, 1, 0, on_vector)
+        quant_w(EVEN, 1, 0)
+        add_squares(0, 0, 256, "plane00")
+        weave_w(EVEN, 1, 1, on_vector)
+        quant_w(EVEN, 1, 1)
+        root(0, 0, 256)
+        turn_and_add(0, 256, 768)
+        root_of_bank(0, 256, 256)
+        root_of_bank(0, 512, 256)
+        root_of_bank(0, 768, 256)
+        weave_w(ODD, 1, 0, on_vector)
+        quant_w(ODD, 1, 0)
+        quant_h(0, 0)
+        weave_w(ODD, 1, 1, on_vector)
+        quant_h(0, 256)
+        quant_w(ODD, 1, 1)
+        by_filter(EVEN, 1, 0, 256)
+        by_filter(EVEN, 1, 256, 256)
+        by_filter(ODD, 1, 0, 256)
+        by_filter(ODD, 1, 256, 256)
+        square_on_vector(EVEN, 1, 256, 256)
+        square(EVEN, 1, 0, 256)
+        square(ODD, 1, 0, 256)
+        square(ODD, 1, 256, 256)
+        by_filter(EVEN, 1, 512, 256)
+        by_filter(ODD, 1, 512, 256)
+        by_filter(EVEN, 1, 768, 128)
+        by_filter(ODD, 1, 768, 128)
+        add_squares(1, 0, 256, "plane01")
+        root(1, 0, 256)
+        add_squares(1, 256, 256, "plane02")
+        square(EVEN, 1, 512, 256)
+        square(ODD, 1, 512, 256)
+        quant_h(1, 0)
+        project(0, 256)
+        by_filter(EVEN, 1, 896, 128)
+        by_filter(ODD, 1, 896, 128)
+        root(1, 256, 256)
+        add_squares(1, 512, 256, "plane03")
+        square_on_vector(EVEN, 1, 768, 128)
+        root(1, 512, 256)
+        square(ODD, 1, 768, 128)
+        square(EVEN, 1, 896, 128)
+        square(ODD, 1, 896, 128)
+        quant_h(1, 256)
+        store(0, 0)
+        store(0, 1)
+        project(256, 256)
+        quant_h(0, 512)
+        quant_h(1, 512)
+        add_squares(1, 768, 128, "plane10")
+        add_squares(1, 896, 128, "plane11")
+        project(512, 256)
+        store(256, 0)
+        root(1, 768, 128)
+        root(1, 896, 128)
+        store(256, 1)
+        quant_h(0, 768)
+        quant_h(1, 768)
+        quant_h(1, 896)
+        store(512, 0)
+        store(512, 1, True)
+        project(768, 128)
+        project(896, 128)
+        store(768, 0)
+        store(768, 1, True)
+        store(896, 0)
+        store(896, 1, True)

@@ -61,9 +61,29 @@ def tile_list_deformable_texture_energy_kernel(tc, xT, wgt, offs, we, wo, wd_wor
             rows = xT[KP * a : KP * (a + 1), :].rearrange("(p i) t -> p i t", i=PACK)
             nc.sync.dma_start(planes[a, i][:], rows[:, i, :])
 
-        def load_gain(hf):
-            gains[hf] = slot([P, W], F32, "gain%d" % hf)
-            nc.sync.dma_start(gains[hf][:], wgt[:, W * hf : W * (hf + 1)])
+        def load_gains():
+            small["chunks"] = slot([P, 64], F32, "chunks")
+            flat = wgt.rearrange("p j -> (p j)")
+            for q in range(4):
+                first = 32 * S * q + S
+                rows = flat[first : first + 32 * (S - 64)].rearrange("(r s) -> r s", s=S - 64)
+                nc.sync.dma_start(small["chunks"][32 * q : 32 * (q + 1), :], rows[:, :64])
+
+        def spread_gains():
+            turned = slot([P, 64], F32, "turned")
+            for e in range(2):
+                nc.vector.transpose(turned[:, 32 * e : 32 * (e + 1)], small["chunks"][:, 32 * e : 32 * (e + 1)])
+            by_chunk = turned[:].rearrange("p (e h c) -> p c e h", e=2, h=2)
+            for hf in range(2):
+                spread = slot([P, W], F32, "spread%d" % hf)
+                dst = spread[:].rearrange("p (k e h r) -> p k e h r", e=2, h=2, r=16)
+                if hf == 0:
+                    nc.vector.tensor_copy(dst[:, 0], by_chunk[:, 0].unsqueeze(3).to_broadcast([P, 2, 2, 16]))
+                    nc.vector.tensor_copy(dst[:, 1:8], by_chunk[:, 15:8:-1].unsqueeze(4).to_broadcast([P, 7, 2, 2, 16]))
+                else:
+                    nc.vector.tensor_copy(dst, by_chunk[:, 8:0:-1].unsqueeze(4).to_broadcast([P, 8, 2, 2, 16]))
+                gains[hf] = slot([P, W], F32, "gain%d" % hf)
+                nc.vector.transpose(gains[hf][:], spread[:])
 
         def load_filter(f, b, a, tag):
             raws[f, b, a] = slot([P, PACK, W], F32, tag)
@@ -247,10 +267,9 @@ def tile_list_deformable_texture_energy_kernel(tc, xT, wgt, offs, we, wo, wd_wor
             nc.sync.dma_start(rows.rearrange("(v p) j -> p v j", p=P), result[:])
 
         on_scalar, on_vector = nc.scalar.copy, nc.vector.tensor_copy
-        load_gain(0)
-        load_plane(0, 0)
-        load_gain(1)
-        for i in range(1, PACK):
+        load_gains()
+        spread_gains()
+        for i in range(PACK):
             load_plane(0, i)
         for i in range(3):
             load_plane(1, i)

@@ -42,7 +42,6 @@ def tile_list_deformable_texture_energy_kernel(tc, xT, wgt, offs, we, wo, wd_wor
             return psum.tile(shape, F32, name="bank%d" % index, tag="bank%d" % index, bufs=1)
 
         offsets = lists.tile([P, S // 16], U16, name="offsets")
-        nc.sync.dma_start(offsets[:], offs)
 
         wd_plane = slot([P, 2, N], U8, "wd_plane")
         nc.gpsimd.memset(wd_plane[:].rearrange("p a n -> p (a n)").bitcast(I32), 0)
@@ -177,7 +176,10 @@ def tile_list_deformable_texture_energy_kernel(tc, xT, wgt, offs, we, wo, wd_wor
 
         def square(f, b, lo, width):
             for at in range(lo, lo + width, P):
-                nc.scalar.activation(room(f, b, at, P), sums[f, b, at][:], ACT.Square)
+                dst, src = room(f, b, at, P), sums[f, b, at][:]
+                if spans.get((b, at)) == (at, P):
+                    dst, src = dst.rearrange("p (j t) -> p j t", t=PACK), src.rearrange("p (t j) -> p j t", t=PACK)
+                nc.scalar.activation(dst, src, ACT.Square)
 
         def square_on_vector(f, b, lo, width):
             plain = {}
@@ -221,6 +223,9 @@ def tile_list_deformable_texture_energy_kernel(tc, xT, wgt, offs, we, wo, wd_wor
 
         def root(b, lo, width):
             woven[b, lo] = slot([P, PACK * width], BF16, "h%d%d" % (b, lo))
+            if width == P:
+                nc.scalar.activation(woven[b, lo][:], totals[b, lo][:], ACT.Sqrt)
+                return
             nc.scalar.activation(
                 woven[b, lo][:].rearrange("p (c j t) -> p c t j", j=4, t=PACK),
                 totals[b, lo][:].rearrange("p (t c j) -> p c t j", j=4, t=PACK),
@@ -264,12 +269,15 @@ def tile_list_deformable_texture_energy_kernel(tc, xT, wgt, offs, we, wo, wd_wor
                 columns = small["bias"][:, first : first + per_bank].unsqueeze(2)
                 nc.vector.tensor_tensor(result[:], acc[:], columns.to_broadcast([P, per_bank, width]), ALU.add)
             rows = out[P * first : P * (first + per_bank), lo : lo + width]
-            nc.sync.dma_start(rows.rearrange("(v p) j -> p v j", p=P), result[:])
+            queue = nc.scalar if on_scalar else nc.sync
+            queue.dma_start(rows.rearrange("(v p) j -> p v j", p=P), result[:])
 
         on_scalar, on_vector = nc.scalar.copy, nc.vector.tensor_copy
         load_gains()
         spread_gains()
-        for i in range(PACK):
+        load_plane(0, 0)
+        nc.sync.dma_start(offsets[:], offs)
+        for i in range(1, PACK):
             load_plane(0, i)
         for i in range(3):
             load_plane(1, i)
@@ -346,7 +354,8 @@ def tile_list_deformable_texture_energy_kernel(tc, xT, wgt, offs, we, wo, wd_wor
         by_filter(EVEN, 1, 256, 256)
         by_filter(ODD, 1, 0, 256)
         by_filter(ODD, 1, 256, 256)
-        square_on_vector(EVEN, 1, 256, 256)
+        square_on_vector(EVEN, 1, 256, 128)
+        square(EVEN, 1, 384, 128)
         square(EVEN, 1, 0, 256)
         square(ODD, 1, 0, 256)
         square(ODD, 1, 256, 256)
@@ -365,7 +374,7 @@ def tile_list_deformable_texture_energy_kernel(tc, xT, wgt, offs, we, wo, wd_wor
         by_filter(ODD, 1, 896, 128)
         root(1, 256, 256)
         add_squares(1, 512, 256, "plane03")
-        square_on_vector(EVEN, 1, 768, 128)
+        square(EVEN, 1, 768, 128)
         root(1, 512, 256)
         square(ODD, 1, 768, 128)
         square(EVEN, 1, 896, 128)

@@ -187,7 +187,11 @@ def tile_list_deformable_texture_energy_kernel(tc, xT, wgt, offs, we, wo, wd_wor
                 plain[at] = slot([P, W], F32, "plain", 2)
                 nc.vector.tensor_copy(plain[at][:], sums[f, b, at][:])
             for at in range(lo, lo + width, P):
-                nc.vector.tensor_tensor(room(f, b, at, P), sums[f, b, at][:], plain[at][:], ALU.mult)
+                dst, src, twin = room(f, b, at, P), sums[f, b, at][:], plain[at][:]
+                if spans.get((b, at)) == (at, P):
+                    dst = dst.rearrange("p (j t) -> p j t", t=PACK)
+                    src, twin = (v.rearrange("p (t j) -> p j t", t=PACK) for v in (src, twin))
+                nc.vector.tensor_tensor(dst, src, twin, ALU.mult)
 
         def turn_and_add(b, lo, width):
             for n in range(width // P):
@@ -315,7 +319,8 @@ def tile_list_deformable_texture_energy_kernel(tc, xT, wgt, offs, we, wo, wd_wor
         weave_x(1, 1, on_scalar)
         quant_x(0, 1)
         quant_w(EVEN, 0, 1)
-        weave_w(ODD, 0, 0, on_vector)
+        weave_w(ODD, 0, 0, on_vector, hi=88)
+        weave_w(ODD, 0, 0, on_scalar, lo=88)
         quant_x(1, 1)
         quant_w(ODD, 0, 0)
         weave_w(ODD, 0, 1, on_vector)
@@ -366,7 +371,8 @@ def tile_list_deformable_texture_energy_kernel(tc, xT, wgt, offs, we, wo, wd_wor
         add_squares(1, 0, 256, "plane01")
         root(1, 0, 256)
         add_squares(1, 256, 256, "plane02")
-        square(EVEN, 1, 512, 256)
+        square_on_vector(EVEN, 1, 640, 128)
+        square(EVEN, 1, 512, 128)
         square(ODD, 1, 512, 256)
         quant_h(1, 0)
         project(0, 256)

@@ -21,7 +21,17 @@ P = 128
 PACK = 4
 KP = P * PACK
 W = 512
+BANKS = 8
+QUAD = 32
+HEAD = 16
+CHUNK = S // HEAD
+QUARTER = 256
 EVEN, ODD = 0, 1
+
+PARTS = ((0, 256), (256, 256), (512, 256), (768, 128), (896, 128))
+SQUARED_ON_VECTOR = ((EVEN, 256), (EVEN, 640))
+SCALAR_GROUPS = 40
+PARTS_SHARED_WITH_SCALAR = 3
 
 
 def tile_list_deformable_texture_energy_kernel(tc, xT, wgt, offs, we, wo, wd_words, wd_scales, bias, out):
@@ -34,14 +44,14 @@ def tile_list_deformable_texture_energy_kernel(tc, xT, wgt, offs, we, wo, wd_wor
         def slot(shape, dtype, tag, bufs=1):
             return keep.tile(shape, dtype, name=tag, tag=tag, bufs=bufs, align_bytes=64)
 
-        taken = []
+        banks_taken = []
 
         def bank(shape):
-            index = len(taken) % 8
-            taken.append(index)
+            index = len(banks_taken) % BANKS
+            banks_taken.append(index)
             return psum.tile(shape, F32, name="bank%d" % index, tag="bank%d" % index, bufs=1)
 
-        offsets = lists.tile([P, S // 16], U16, name="offsets")
+        offsets = lists.tile([P, S // HEAD], U16, name="offsets")
 
         wd_plane = slot([P, 2, N], U8, "wd_plane")
         nc.gpsimd.memset(wd_plane[:].rearrange("p a n -> p (a n)").bitcast(I32), 0)
@@ -52,91 +62,94 @@ def tile_list_deformable_texture_energy_kernel(tc, xT, wgt, offs, we, wo, wd_wor
         nc.vector.memset(warm[:, 0:1], 1.0)
         nc.scalar.activation(warm[:, 1:2], warm[:, 0:1], ACT.Sqrt)
 
-        planes, gains, raws, small, spans = {}, {}, {}, {}, {}
-        xq, wq, hq, picked, squares, woven, totals, sums, results = {}, {}, {}, {}, {}, {}, {}, {}, {}
+        on_scalar, on_vector = nc.scalar.copy, nc.vector.tensor_copy
+        planes, gains, pieces, picked, woven = {}, {}, {}, {}, {}
+        xq, wq, hq = {}, {}, {}
+        sums, slices, squares, totals = {}, {}, {}, {}
+
+        def load_gains():
+            chunks = slot([P, CHUNK], F32, "chunks")
+            flat = wgt.rearrange("p j -> (p j)")
+            for q in range(P // QUAD):
+                first = QUAD * S * q + S
+                rows = flat[first : first + QUAD * (S - CHUNK)].rearrange("(r s) -> r s", s=S - CHUNK)
+                nc.sync.dma_start(chunks[QUAD * q : QUAD * (q + 1), :], rows[:, :CHUNK])
+            turned = slot([P, CHUNK], F32, "turned")
+            for e in range(CHUNK // QUAD):
+                nc.vector.transpose(turned[:, QUAD * e : QUAD * (e + 1)], chunks[:, QUAD * e : QUAD * (e + 1)])
+            by_source = turned[:].rearrange("p (e h c) -> p c e h", e=2, h=2).unsqueeze(4)
+            for hf, runs in enumerate(
+                (
+                    ((0, 1, slice(0, 1), on_vector), (1, 8, slice(15, 8, -1), on_vector)),
+                    ((0, 8, slice(8, 0, -1), on_scalar),),
+                )
+            ):
+                spread = slot([P, W], F32, "spread%d" % hf)
+                by_chunk = spread[:].rearrange("p (k e h r) -> p k e h r", e=2, h=2, r=HEAD)
+                for lo, hi, sources, copy in runs:
+                    copy(by_chunk[:, lo:hi], by_source[:, sources].to_broadcast([P, hi - lo, 2, 2, HEAD]))
+                gains[hf] = slot([P, W], F32, "gain%d" % hf)
+                nc.vector.transpose(gains[hf][:], spread[:])
 
         def load_plane(a, i):
             planes[a, i] = slot([P, T], F32, "plane%d%d" % (a, i))
             rows = xT[KP * a : KP * (a + 1), :].rearrange("(p i) t -> p i t", i=PACK)
             nc.sync.dma_start(planes[a, i][:], rows[:, i, :])
 
-        def load_gains():
-            small["chunks"] = slot([P, 64], F32, "chunks")
-            flat = wgt.rearrange("p j -> (p j)")
-            for q in range(4):
-                first = 32 * S * q + S
-                rows = flat[first : first + 32 * (S - 64)].rearrange("(r s) -> r s", s=S - 64)
-                nc.sync.dma_start(small["chunks"][32 * q : 32 * (q + 1), :], rows[:, :64])
-
-        def spread_gains():
-            turned = slot([P, 64], F32, "turned")
-            for e in range(2):
-                nc.vector.transpose(turned[:, 32 * e : 32 * (e + 1)], small["chunks"][:, 32 * e : 32 * (e + 1)])
-            by_chunk = turned[:].rearrange("p (e h c) -> p c e h", e=2, h=2)
-            for hf in range(2):
-                spread = slot([P, W], F32, "spread%d" % hf)
-                dst = spread[:].rearrange("p (k e h r) -> p k e h r", e=2, h=2, r=16)
-                if hf == 0:
-                    nc.vector.tensor_copy(dst[:, 0], by_chunk[:, 0].unsqueeze(3).to_broadcast([P, 2, 2, 16]))
-                    nc.vector.tensor_copy(dst[:, 1:8], by_chunk[:, 15:8:-1].unsqueeze(4).to_broadcast([P, 7, 2, 2, 16]))
-                else:
-                    nc.vector.tensor_copy(dst, by_chunk[:, 8:0:-1].unsqueeze(4).to_broadcast([P, 8, 2, 2, 16]))
-                gains[hf] = slot([P, W], F32, "gain%d" % hf)
-                nc.vector.transpose(gains[hf][:], spread[:])
-
-        def load_filter(f, b, a, tag):
-            raws[f, b, a] = slot([P, PACK, W], F32, tag)
+        def load_piece(f, b, a, tag):
+            pieces[f, b, a] = slot([P, PACK, W], F32, tag)
             rows = (we, wo)[f][KP * a : KP * (a + 1), W * b : W * (b + 1)]
-            nc.sync.dma_start(raws[f, b, a][:], rows.rearrange("(p i) c -> p i c", i=PACK))
+            nc.sync.dma_start(pieces[f, b, a][:], rows.rearrange("(p i) c -> p i c", i=PACK))
 
-        def load_small():
-            small["wd"] = slot([P, 2, 2 * N], U8, "wd_codes")
-            nc.sync.dma_start(small["wd"][:].bitcast(I32), wd_words.rearrange("a p c -> p a c").bitcast(I32))
-            for q in range(4):
+        def load_last_stage():
+            words = slot([P, 2, 2 * N], U8, "wd_words")
+            nc.sync.dma_start(words[:].bitcast(I32), wd_words.rearrange("a p c -> p a c").bitcast(I32))
+            for q in range(P // QUAD):
                 nc.sync.dma_start(
-                    wd_plane[32 * q : 32 * q + 4, :, :].bitcast(I32),
+                    wd_plane[QUAD * q : QUAD * q + 4, :, :].bitcast(I32),
                     wd_scales[:, 4 * q : 4 * q + 4, :].rearrange("a r n -> r a n").bitcast(I32),
                 )
-            small["bias"] = slot([P, N // P], F32, "bias_cols")
+            columns = slot([P, N // P], F32, "bias_columns")
             with nc.allow_non_contiguous_dma(reason="one bias value a partition"):
-                nc.sync.dma_start(small["bias"][:], bias.rearrange("(u p) -> p u", p=P))
+                nc.sync.dma_start(columns[:], bias.rearrange("(u p) -> p u", p=P))
+            return words, columns
 
-        def quantise(grouped, name):
-            width = grouped.shape[1] // PACK
+        def quantise(values, name):
+            width = values.shape[1] // PACK
             codes = slot([P, width], U32, name + "c")
             scales = slot([P, width], U8, name + "s")
-            nc.vector.quantize_mx(out=codes[:].bitcast(FP8X4), scales=scales[:], in_=grouped)
+            nc.vector.quantize_mx(out=codes[:].bitcast(FP8X4), scales=scales[:], in_=values[:])
             return codes, scales
 
         def gather(hf, a, i, lo=0, width=W):
             if (i, lo) == (0, 0):
                 picked[hf, a] = slot([P, PACK, W], F32, "picked%d%d" % (hf, a))
-            cut = offsets[:, (hf * W + lo) // 16 : (hf * W + lo + width) // 16]
+            cut = offsets[:, (hf * W + lo) // HEAD : (hf * W + lo + width) // HEAD]
             nc.vector.tensor_tensor(
                 picked[hf, a][:, i, lo : lo + width], planes[a, i][:].indirect(cut), gains[hf][:, lo : lo + width], ALU.mult
             )
 
-        def weave_x(hf, a, copy, lo=0, width=W, tag="xgrp", bufs=2):
+        def weave_x(hf, a, lo=0, width=W):
             if lo == 0:
-                woven["x", hf, a] = slot([P, PACK * W], BF16, tag, bufs)
-            copy(
+                woven["x", hf, a] = slot([P, PACK * W], BF16, "woven_x", 2)
+            on_scalar(
                 woven["x", hf, a][:, PACK * lo : PACK * (lo + width)].rearrange("p (c j i) -> p c i j", j=4, i=PACK),
                 picked[hf, a][:, :, lo : lo + width].rearrange("p i (c j) -> p c i j", j=4),
             )
 
-        def quant_x(hf, a):
-            xq[hf, a] = quantise(woven["x", hf, a][:], "xq%d%d" % (hf, a))
+        def quantise_x(hf, a):
+            xq[hf, a] = quantise(woven["x", hf, a], "xq%d%d" % (hf, a))
 
-        def weave_w(f, b, a, copy, tag="wgrp", bufs=3, lo=0, hi=P):
+        def weave_piece(f, b, a, copy, lo=0, hi=P):
             if lo == 0:
-                woven["w", f, b, a] = slot([P, PACK * W], BF16, tag, bufs)
+                woven["w", f, b, a] = slot([P, PACK * W], BF16, "woven_w", 3)
             copy(
                 woven["w", f, b, a][:].rearrange("p (t m i) -> p m i t", t=PACK, i=PACK)[:, lo:hi],
-                raws[f, b, a][:].rearrange("p i (m t) -> p m i t", t=PACK)[:, lo:hi],
+                pieces[f, b, a][:].rearrange("p i (m t) -> p m i t", t=PACK)[:, lo:hi],
             )
 
-        def quant_w(f, b, a):
-            wq[f, b, a] = quantise(woven["w", f, b, a][:], "wq%d%d%d" % (f, b, a))
+        def quantise_piece(f, b, a):
+            wq[f, b, a] = quantise(woven["w", f, b, a], "wq%d%d%d" % (f, b, a))
 
         def mx_pass(acc, stationary, at, moving, lo, width, start, stop):
             nc.tensor.matmul_mx(
@@ -149,263 +162,225 @@ def tile_list_deformable_texture_energy_kernel(tc, xT, wgt, offs, we, wo, wd_wor
                 stop=stop,
             )
 
-        def room(f, b, lo, width):
-            return squares[f, b, lo // W][:, PACK * (lo % W) : PACK * (lo % W + width)]
-
-        def by_query(f, b, lo, width, passes=(0, 1)):
+        def respond_by_query(f, b, lo, width, passes=(0, 1)):
             for at in range(lo, lo + width, P):
                 for a in passes:
                     if a == 0:
                         sums[f, b, at] = bank([P, W])
+                        slices[b, at] = 1
                     mx_pass(sums[f, b, at][:], xq[at // W, a], at % W, wq[f, b, a], 0, W, a == 0, a == 1)
 
-        def by_filter(f, b, lo, width, passes=(0, 1)):
+        def respond_by_filter(f, b, lo, width, passes=(0, 1)):
             per_bank = W // width
-            for at in range(lo, lo + width, P):
-                spans[b, at] = (lo, width)
             for n in range(PACK // per_bank):
+                key = lo + P * n
                 for a in passes:
                     if a == 0:
-                        sums[f, b, lo + P * n] = bank([P, W])
+                        sums[f, b, key] = bank([P, W])
+                        slices[b, key] = per_bank
                     for v in range(per_bank):
                         mx_pass(
-                            sums[f, b, lo + P * n][:, width * v : width * (v + 1)],
-                            wq[f, b, a], P * (per_bank * n + v), xq[lo // W, a], lo % W, width,
-                            (a, v) == (0, 0), (a, v) == (1, per_bank - 1),
+                            sums[f, b, key][:, width * v : width * (v + 1)],
+                            wq[f, b, a],
+                            P * (per_bank * n + v),
+                            xq[lo // W, a],
+                            lo % W,
+                            width,
+                            (a, v) == (0, 0),
+                            (a, v) == (1, per_bank - 1),
                         )
 
-        def square(f, b, lo, width):
-            for at in range(lo, lo + width, P):
-                dst, src = room(f, b, at, P), sums[f, b, at][:]
-                if spans.get((b, at)) == (at, P):
-                    dst, src = dst.rearrange("p (j t) -> p j t", t=PACK), src.rearrange("p (t j) -> p j t", t=PACK)
+        def squares_of(f, b, lo, width):
+            return squares[f, b, lo // W][:, PACK * (lo % W) : PACK * (lo % W + width)]
+
+        def square(f, b, key):
+            dst, src = squares_of(f, b, key, P), sums[f, b, key][:]
+            if b == 1 and (f, key) in SQUARED_ON_VECTOR:
+                twin = slot([P, W], F32, "twin", 2)
+                nc.vector.tensor_copy(twin[:], src)
+                nc.vector.tensor_tensor(dst, src, twin[:], ALU.mult)
+            elif slices[b, key] == PACK:
+                nc.scalar.activation(
+                    dst.rearrange("p (j t) -> p j t", t=PACK), src.rearrange("p (t j) -> p j t", t=PACK), ACT.Square
+                )
+            else:
                 nc.scalar.activation(dst, src, ACT.Square)
 
-        def square_on_vector(f, b, lo, width):
-            plain = {}
-            for at in range(lo, lo + width, P):
-                plain[at] = slot([P, W], F32, "plain", 2)
-                nc.vector.tensor_copy(plain[at][:], sums[f, b, at][:])
-            for at in range(lo, lo + width, P):
-                dst, src, twin = room(f, b, at, P), sums[f, b, at][:], plain[at][:]
-                if spans.get((b, at)) == (at, P):
-                    dst = dst.rearrange("p (j t) -> p j t", t=PACK)
-                    src, twin = (v.rearrange("p (t j) -> p j t", t=PACK) for v in (src, twin))
-                nc.vector.tensor_tensor(dst, src, twin, ALU.mult)
+        def square_all(f, b, lo, width):
+            keys = range(lo, lo + width, P)
+            for key in sorted(keys, key=lambda k: (b, (f, k) in SQUARED_ON_VECTOR) != (1, True)):
+                square(f, b, key)
 
         def turn_and_add(b, lo, width):
-            for n in range(width // P):
-                totals[b, lo + P * n] = bank([P, PACK, P])
+            for at in range(lo, lo + width, P):
+                totals[b, at] = bank([P, PACK, P])
                 for t in range(PACK):
                     for f in (EVEN, ODD):
                         nc.tensor.matmul(
-                            totals[b, lo + P * n][:, t, :],
-                            lhsT=room(f, b, lo + P * n, P)[:, P * t : P * (t + 1)],
+                            totals[b, at][:, t, :],
+                            lhsT=squares_of(f, b, at, P)[:, P * t : P * (t + 1)],
                             rhs=identity[:],
                             start=(f == EVEN),
                             stop=(f == ODD),
                             is_transpose=True,
                         )
 
-        def root_of_bank(b, lo, width):
-            woven[b, lo] = slot([P, PACK * width], BF16, "h%d%d" % (b, lo))
-            for n in range(width // P):
+        def root_of_banks(b, lo, width):
+            woven["h", b, lo] = slot([P, PACK * width], BF16, "h%d%d" % (b, lo))
+            for at in range(lo, lo + width, P):
                 nc.scalar.activation(
-                    woven[b, lo][:, W * n : W * (n + 1)].rearrange("p (j t) -> p j t", t=PACK),
-                    totals[b, lo + P * n][:].rearrange("p t j -> p j t"),
+                    woven["h", b, lo][:, PACK * (at - lo) : PACK * (at - lo + P)].rearrange("p (j t) -> p j t", t=PACK),
+                    totals[b, at][:].rearrange("p t j -> p j t"),
                     ACT.Sqrt,
                 )
 
-        def add_squares(b, lo, width, tag, engine=nc.vector):
+        def add_squares(b, lo, width, tag):
             totals[b, lo] = slot([P, PACK * width], F32, tag)
-            start, span = spans[b, lo]
-            even, odd = (
-                room(f, b, start, span).rearrange("p (t j) -> p t j", t=PACK)[:, :, lo - start : lo - start + width]
-                for f in (EVEN, ODD)
-            )
-            engine.tensor_tensor(totals[b, lo][:].rearrange("p (t j) -> p t j", t=PACK), even, odd, ALU.add)
+            nc.vector.tensor_tensor(totals[b, lo][:], squares_of(EVEN, b, lo, width), squares_of(ODD, b, lo, width), ALU.add)
 
         def root(b, lo, width):
-            woven[b, lo] = slot([P, PACK * width], BF16, "h%d%d" % (b, lo))
-            if width == P:
-                nc.scalar.activation(woven[b, lo][:], totals[b, lo][:], ACT.Sqrt)
-                return
-            nc.scalar.activation(
-                woven[b, lo][:].rearrange("p (c j t) -> p c t j", j=4, t=PACK),
-                totals[b, lo][:].rearrange("p (t c j) -> p c t j", j=4, t=PACK),
-                ACT.Sqrt,
-            )
+            woven["h", b, lo] = slot([P, PACK * width], BF16, "h%d%d" % (b, lo))
+            dst, src = woven["h", b, lo][:], totals[b, lo][:]
+            if slices[b, lo] != PACK:
+                dst = dst.rearrange("p (c j t) -> p c t j", j=4, t=PACK)
+                src = src.rearrange("p (t c j) -> p c t j", j=4, t=PACK)
+            nc.scalar.activation(dst, src, ACT.Sqrt)
 
-        def quant_h(b, lo):
-            codes, scales = quantise(woven[b, lo][:], "hq%d%d" % (b, lo))
+        def quantise_h(b, lo):
+            codes, scales = quantise(woven["h", b, lo], "hq%d%d" % (b, lo))
             for at in range(0, codes.shape[1], P):
                 hq[b, lo + at] = (codes, scales, at)
 
-        def project(lo, width, blocks=(0, 1)):
-            per_bank = 2
-            for n in range(N // P // per_bank):
-                for b in blocks:
-                    if b == 0:
-                        sums["out", lo, n] = bank([P, per_bank, width])
+        def project(lo, width):
+            for n in range(2):
+                sums["out", lo, n] = bank([P, 2, width])
+                for b in range(2):
                     codes, scales, at = hq[b, lo]
-                    for v in range(per_bank):
-                        u = per_bank * n + v
+                    for v in range(2):
+                        u = 2 * n + v
                         nc.tensor.matmul_mx(
                             sums["out", lo, n][:, v, :],
-                            lhsT=small["wd"][:, b, 2 * P * u : 2 * P * (u + 1)].bitcast(FP4X4),
+                            lhsT=wd_codes[:, b, 2 * P * u : 2 * P * (u + 1)].bitcast(FP4X4),
                             lhsT_scale=wd_plane[:, b, P * u : P * (u + 1)],
                             rhs=codes[:, at : at + width].bitcast(FP8X4),
                             rhs_scale=scales[:, at : at + width],
                             start=((b, v) == (0, 0)),
-                            stop=((b, v) == (1, per_bank - 1)),
+                            stop=((b, v) == (1, 1)),
                         )
 
-        def store(lo, n, on_scalar=False):
+        def store(lo, width, n, by_scalar):
             acc = sums["out", lo, n]
-            per_bank, width = acc.shape[1], acc.shape[2]
-            first = per_bank * n
-            result = slot([P, per_bank, width], F32, "result", 10)
-            if on_scalar:
-                for v in range(per_bank):
-                    column = small["bias"][:, first + v : first + v + 1]
+            result = slot([P, 2, width], F32, "result", 10)
+            if by_scalar:
+                for v in range(2):
+                    column = bias_columns[:, 2 * n + v : 2 * n + v + 1]
                     nc.scalar.activation(result[:, v, :], acc[:, v, :], ACT.Identity, bias=column)
             else:
-                columns = small["bias"][:, first : first + per_bank].unsqueeze(2)
-                nc.vector.tensor_tensor(result[:], acc[:], columns.to_broadcast([P, per_bank, width]), ALU.add)
-            rows = out[P * first : P * (first + per_bank), lo : lo + width]
-            queue = nc.scalar if on_scalar else nc.sync
+                columns = bias_columns[:, 2 * n : 2 * n + 2].unsqueeze(2)
+                nc.vector.tensor_tensor(result[:], acc[:], columns.to_broadcast([P, 2, width]), ALU.add)
+            rows = out[2 * P * n : 2 * P * (n + 1), lo : lo + width]
+            queue = nc.scalar if by_scalar else nc.sync
             queue.dma_start(rows.rearrange("(v p) j -> p v j", p=P), result[:])
 
-        on_scalar, on_vector = nc.scalar.copy, nc.vector.tensor_copy
         load_gains()
-        spread_gains()
         load_plane(0, 0)
         nc.sync.dma_start(offsets[:], offs)
-        for i in range(1, PACK):
-            load_plane(0, i)
-        for i in range(3):
-            load_plane(1, i)
-        load_filter(EVEN, 0, 0, "first")
-        load_plane(1, 3)
-        load_filter(EVEN, 0, 1, "second")
+        for a, i in [(a, i) for a in range(2) for i in range(PACK)][1:-1]:
+            load_plane(a, i)
+        load_piece(EVEN, 0, 0, "first")
+        load_plane(1, PACK - 1)
+        load_piece(EVEN, 0, 1, "second")
+
         for i in range(PACK):
-            gather(0, 0, i)
-            gather(1, 0, i)
-        load_filter(ODD, 0, 0, "plane00")
-        load_filter(ODD, 0, 1, "plane01")
-        load_filter(EVEN, 1, 0, "plane02")
-        load_filter(EVEN, 1, 1, "plane03")
-        weave_x(0, 0, on_scalar)
-        weave_x(1, 0, on_scalar)
-        gather(0, 1, 0)
-        gather(1, 1, 0)
-        quant_x(0, 0)
-        gather(0, 1, 1)
-        gather(1, 1, 1)
-        quant_x(1, 0)
-        gather(0, 1, 2)
-        gather(1, 1, 2)
-        load_filter(ODD, 1, 0, "plane10")
-        load_filter(ODD, 1, 1, "plane11")
-        load_small()
-        weave_w(EVEN, 0, 0, on_scalar)
-        gather(0, 1, 3, 0, 256)
-        gather(0, 1, 3, 256, 256)
-        weave_x(0, 1, on_scalar, 0, 256)
-        weave_x(0, 1, on_scalar, 256, 256)
-        quant_w(EVEN, 0, 0)
-        gather(1, 1, 3)
-        weave_w(EVEN, 0, 1, on_vector)
-        weave_x(1, 1, on_scalar)
-        quant_x(0, 1)
-        quant_w(EVEN, 0, 1)
-        weave_w(ODD, 0, 0, on_vector, hi=88)
-        weave_w(ODD, 0, 0, on_scalar, lo=88)
-        quant_x(1, 1)
-        quant_w(ODD, 0, 0)
-        weave_w(ODD, 0, 1, on_vector)
-        quant_w(ODD, 0, 1)
-        for f, hf, tag in ((EVEN, 0, "picked00"), (EVEN, 1, "picked10"), (ODD, 0, "first"), (ODD, 1, "plane12")):
-            squares[f, 0, hf] = slot([P, PACK * W], F32, tag)
-        for f, hf, tag in ((EVEN, 0, "plane13"), (EVEN, 1, "picked01"), (ODD, 0, "picked11"), (ODD, 1, "second")):
-            squares[f, 1, hf] = slot([P, PACK * W], F32, tag)
-        for passes in ((0,), (1,)):
-            by_filter(EVEN, 0, 0, 256, passes)
-            by_query(EVEN, 0, 256, 768, passes)
-        square(EVEN, 0, 0, 1024)
-        by_filter(ODD, 0, 0, 256, (0,))
-        by_query(ODD, 0, 256, 256, (0,))
-        by_filter(ODD, 0, 0, 256, (1,))
-        by_query(ODD, 0, 256, 256, (1,))
-        by_query(ODD, 0, 512, 512)
-        square(ODD, 0, 0, 1024)
-        weave_w(EVEN, 1, 0, on_vector)
-        quant_w(EVEN, 1, 0)
-        add_squares(0, 0, 256, "plane00")
-        weave_w(EVEN, 1, 1, on_vector)
-        quant_w(EVEN, 1, 1)
-        root(0, 0, 256)
-        turn_and_add(0, 256, 768)
-        root_of_bank(0, 256, 256)
-        root_of_bank(0, 512, 256)
-        root_of_bank(0, 768, 256)
-        weave_w(ODD, 1, 0, on_vector)
-        quant_w(ODD, 1, 0)
-        quant_h(0, 0)
-        weave_w(ODD, 1, 1, on_vector)
-        quant_h(0, 256)
-        quant_w(ODD, 1, 1)
-        by_filter(EVEN, 1, 0, 256)
-        by_filter(EVEN, 1, 256, 256)
-        by_filter(ODD, 1, 0, 256)
-        by_filter(ODD, 1, 256, 256)
-        square_on_vector(EVEN, 1, 256, 128)
-        square(EVEN, 1, 384, 128)
-        square(EVEN, 1, 0, 256)
-        square(ODD, 1, 0, 256)
-        square(ODD, 1, 256, 256)
-        by_filter(EVEN, 1, 512, 256)
-        by_filter(ODD, 1, 512, 256)
-        by_filter(EVEN, 1, 768, 128)
-        by_filter(ODD, 1, 768, 128)
-        add_squares(1, 0, 256, "plane01")
-        root(1, 0, 256)
-        add_squares(1, 256, 256, "plane02")
-        square_on_vector(EVEN, 1, 640, 128)
-        square(EVEN, 1, 512, 128)
-        square(ODD, 1, 512, 256)
-        quant_h(1, 0)
-        project(0, 256)
-        by_filter(EVEN, 1, 896, 128)
-        by_filter(ODD, 1, 896, 128)
-        root(1, 256, 256)
-        add_squares(1, 512, 256, "plane03")
-        square(EVEN, 1, 768, 128)
-        root(1, 512, 256)
-        square(ODD, 1, 768, 128)
-        square(EVEN, 1, 896, 128)
-        square(ODD, 1, 896, 128)
-        quant_h(1, 256)
-        store(0, 0)
-        store(0, 1)
-        project(256, 256)
-        quant_h(0, 512)
-        quant_h(1, 512)
-        add_squares(1, 768, 128, "plane10")
-        add_squares(1, 896, 128, "plane11")
-        project(512, 256)
-        store(256, 0)
-        root(1, 768, 128)
-        root(1, 896, 128)
-        store(256, 1)
-        quant_h(0, 768)
-        quant_h(1, 768)
-        quant_h(1, 896)
-        store(512, 0)
-        store(512, 1, True)
-        project(768, 128)
-        project(896, 128)
-        store(768, 0)
-        store(768, 1, True)
-        store(896, 0)
-        store(896, 1, True)
+            for hf in range(2):
+                gather(hf, 0, i)
+        for i, (f, b, a) in enumerate(((ODD, 0, 0), (ODD, 0, 1), (EVEN, 1, 0), (EVEN, 1, 1))):
+            load_piece(f, b, a, "plane0%d" % i)
+        for hf in range(2):
+            weave_x(hf, 0)
+        for i in range(PACK - 1):
+            for hf in range(2):
+                gather(hf, 1, i)
+            if i < 2:
+                quantise_x(i, 0)
+        for a in range(2):
+            load_piece(ODD, 1, a, "plane1%d" % a)
+        wd_codes, bias_columns = load_last_stage()
+
+        weave_piece(EVEN, 0, 0, on_scalar)
+        for lo in (0, QUARTER):
+            gather(0, 1, PACK - 1, lo, QUARTER)
+        for lo in (0, QUARTER):
+            weave_x(0, 1, lo, QUARTER)
+        quantise_piece(EVEN, 0, 0)
+        gather(1, 1, PACK - 1)
+        weave_piece(EVEN, 0, 1, on_vector)
+        weave_x(1, 1)
+        quantise_x(0, 1)
+        quantise_piece(EVEN, 0, 1)
+        weave_piece(ODD, 0, 0, on_vector, 0, P - SCALAR_GROUPS)
+        weave_piece(ODD, 0, 0, on_scalar, P - SCALAR_GROUPS, P)
+        quantise_x(1, 1)
+        quantise_piece(ODD, 0, 0)
+        weave_piece(ODD, 0, 1, on_vector)
+        quantise_piece(ODD, 0, 1)
+
+        homes = (("picked00", "picked10", "first", "plane12"), ("plane13", "picked01", "picked11", "second"))
+        for b in range(2):
+            for f in (EVEN, ODD):
+                for hf in range(2):
+                    squares[f, b, hf] = slot([P, PACK * W], F32, homes[b][2 * f + hf])
+
+        for a in range(2):
+            respond_by_filter(EVEN, 0, 0, QUARTER, (a,))
+            respond_by_query(EVEN, 0, QUARTER, S - QUARTER, (a,))
+        square_all(EVEN, 0, 0, S)
+        for a in range(2):
+            respond_by_filter(ODD, 0, 0, QUARTER, (a,))
+            respond_by_query(ODD, 0, QUARTER, QUARTER, (a,))
+        respond_by_query(ODD, 0, W, W)
+        square_all(ODD, 0, 0, S)
+        weave_piece(EVEN, 1, 0, on_vector)
+        quantise_piece(EVEN, 1, 0)
+        add_squares(0, 0, QUARTER, "plane00")
+        weave_piece(EVEN, 1, 1, on_vector)
+        quantise_piece(EVEN, 1, 1)
+        root(0, 0, QUARTER)
+        turn_and_add(0, QUARTER, S - QUARTER)
+        for lo in range(QUARTER, S, QUARTER):
+            root_of_banks(0, lo, QUARTER)
+        weave_piece(ODD, 1, 0, on_vector)
+        quantise_piece(ODD, 1, 0)
+        quantise_h(0, 0)
+        weave_piece(ODD, 1, 1, on_vector)
+        quantise_h(0, QUARTER)
+        quantise_piece(ODD, 1, 1)
+
+        total_homes = ("plane01", "plane02", "plane03", "plane10", "plane11")
+        for step in (respond_by_filter, square_all):
+            for f in (EVEN, ODD):
+                for lo, width in PARTS[:2]:
+                    step(f, 1, lo, width)
+        for f in (EVEN, ODD):
+            respond_by_filter(f, 1, *PARTS[2])
+        add_squares(1, *PARTS[0], total_homes[0])
+        for k in range(len(PARTS) + 1):
+            for lo, width in PARTS[k + 3 : k + 4]:
+                for f in (EVEN, ODD):
+                    respond_by_filter(f, 1, lo, width)
+            for lo, width in PARTS[k : k + 1]:
+                root(1, lo, width)
+            for lo, width in PARTS[k + 1 : k + 2]:
+                add_squares(1, lo, width, total_homes[k + 1])
+            for lo, width in PARTS[k + 2 : k + 3]:
+                for f in (EVEN, ODD):
+                    square_all(f, 1, lo, width)
+            for lo, width in PARTS[k : k + 1]:
+                if (0, lo) not in hq:
+                    quantise_h(0, lo)
+                quantise_h(1, lo)
+                project(lo, width)
+            if k > 0:
+                lo, width = PARTS[k - 1]
+                for n in range(2):
+                    store(lo, width, n, n == 1 and k > len(PARTS) - PARTS_SHARED_WITH_SCALAR)

@@ -81,7 +81,7 @@ def tile_list_deformable_texture_energy_kernel(tc, xT, wgt, offs, we, wo, wd_wor
             for hf, runs in enumerate(
                 (
                     ((0, 1, slice(0, 1), on_vector), (1, 8, slice(15, 8, -1), on_vector)),
-                    ((0, 8, slice(8, 0, -1), on_scalar),),
+                    ((0, 8, slice(8, 0, -1), on_vector),),
                 )
             ):
                 spread = slot([P, W], F32, "spread%d" % hf)

@@ -148,6 +148,20 @@ def tile_list_deformable_texture_energy_kernel(tc, xT, wgt, offs, we, wo, wd_wor
                 pieces[f, b, a][:].rearrange("p i (m t) -> p m i t", t=PACK)[:, lo:hi],
             )
 
+        def prepare_piece(f, b, a):
+            codes = slot([P, W], U32, "wq%d%d%dc" % (f, b, a))
+            scales = slot([P, W], U8, "wq%d%d%ds" % (f, b, a))
+            wq[f, b, a] = (codes, scales)
+            halves = [slot([P, 2 * W], BF16, "woven_half", 4) for u in range(2)]
+            for u in range(2):
+                on_vector(
+                    halves[u][:].rearrange("p (t m i) -> p m i t", t=2, i=PACK),
+                    pieces[f, b, a][:].rearrange("p i (m t) -> p m i t", t=PACK)[:, :, :, 2 * u : 2 * u + 2],
+                )
+            for u in range(2):
+                cut = slice(2 * P * u, 2 * P * (u + 1))
+                nc.vector.quantize_mx(out=codes[:, cut].bitcast(FP8X4), scales=scales[:, cut], in_=halves[u][:])
+
         def quantise_piece(f, b, a):
             wq[f, b, a] = quantise(woven["w", f, b, a], "wq%d%d%d" % (f, b, a))
 
@@ -322,8 +336,7 @@ def tile_list_deformable_texture_energy_kernel(tc, xT, wgt, offs, we, wo, wd_wor
         weave_piece(ODD, 0, 0, on_scalar, P - SCALAR_GROUPS, P)
         quantise_x(1, 1)
         quantise_piece(ODD, 0, 0)
-        weave_piece(ODD, 0, 1, on_vector)
-        quantise_piece(ODD, 0, 1)
+        prepare_piece(ODD, 0, 1)
 
         homes = (("picked00", "picked10", "first", "plane12"), ("plane13", "picked01", "picked11", "second"))
         for b in range(2):
@@ -340,21 +353,17 @@ def tile_list_deformable_texture_energy_kernel(tc, xT, wgt, offs, we, wo, wd_wor
             respond_by_query(ODD, 0, QUARTER, QUARTER, (a,))
         respond_by_query(ODD, 0, W, W)
         square_all(ODD, 0, 0, S)
-        weave_piece(EVEN, 1, 0, on_vector)
-        quantise_piece(EVEN, 1, 0)
+        prepare_piece(EVEN, 1, 0)
         add_squares(0, 0, QUARTER, "plane00")
-        weave_piece(EVEN, 1, 1, on_vector)
-        quantise_piece(EVEN, 1, 1)
+        prepare_piece(EVEN, 1, 1)
         root(0, 0, QUARTER)
         turn_and_add(0, QUARTER, S - QUARTER)
         for lo in range(QUARTER, S, QUARTER):
             root_of_banks(0, lo, QUARTER)
-        weave_piece(ODD, 1, 0, on_vector)
-        quantise_piece(ODD, 1, 0)
+        prepare_piece(ODD, 1, 0)
         quantise_h(0, 0)
-        weave_piece(ODD, 1, 1, on_vector)
+        prepare_piece(ODD, 1, 1)
         quantise_h(0, QUARTER)
-        quantise_piece(ODD, 1, 1)
 
         total_homes = ("plane01", "plane02", "plane03", "plane10", "plane11")
         for step in (respond_by_filter, square_all):

@@ -211,8 +211,11 @@ def tile_list_deformable_texture_energy_kernel(tc, xT, wgt, offs, we, wo, wd_wor
             dst, src = squares_of(f, b, key, P), sums[f, b, key][:]
             if b == 1 and (f, key) in SQUARED_ON_VECTOR:
                 twin = slot([P, W], F32, "twin", 2)
-                nc.vector.tensor_copy(twin[:], src)
-                nc.vector.tensor_tensor(dst, src, twin[:], ALU.mult)
+                cuts = (slice(0, W // 2), slice(W // 2, W))
+                for cut in cuts:
+                    nc.vector.tensor_copy(twin[:, cut], src[:, cut])
+                for cut in cuts:
+                    nc.vector.tensor_tensor(dst[:, cut], src[:, cut], twin[:, cut], ALU.mult)
             elif slices[b, key] == PACK:
                 nc.scalar.activation(
                     dst.rearrange("p (j t) -> p j t", t=PACK), src.rearrange("p (t j) -> p j t", t=PACK), ACT.Square

@@ -30,7 +30,7 @@ EVEN, ODD = 0, 1
 
 PARTS = ((0, 256), (256, 256), (512, 256), (768, 128), (896, 128))
 SQUARED_ON_VECTOR = ((EVEN, 256), (EVEN, 640))
-SCALAR_GROUPS = 40
+SCALAR_GROUPS = 20
 PARTS_SHARED_WITH_SCALAR = 3
 
 
@@ -137,16 +137,22 @@ def tile_list_deformable_texture_energy_kernel(tc, xT, wgt, offs, we, wo, wd_wor
                 picked[hf, a][:, :, lo : lo + width].rearrange("p i (c j) -> p c i j", j=4),
             )
 
-        def quantise_x(hf, a):
-            xq[hf, a] = quantise(woven["x", hf, a], "xq%d%d" % (hf, a))
+        def quantise_x(hf, a, lo=0, width=W):
+            if lo == 0:
+                xq[hf, a] = (slot([P, W], U32, "xq%d%dc" % (hf, a)), slot([P, W], U8, "xq%d%ds" % (hf, a)))
+            codes, scales = xq[hf, a]
+            values = woven["x", hf, a][:, PACK * lo : PACK * (lo + width)]
+            cut = slice(lo, lo + width)
+            nc.vector.quantize_mx(out=codes[:, cut].bitcast(FP8X4), scales=scales[:, cut], in_=values)
 
-        def weave_piece(f, b, a, copy, lo=0, hi=P):
+        def weave_piece(f, b, a, copy, slices_at_once, lo=0, hi=P):
             if lo == 0:
                 woven["w", f, b, a] = slot([P, PACK * W], BF16, "woven_w", 3)
-            copy(
-                woven["w", f, b, a][:].rearrange("p (t m i) -> p m i t", t=PACK, i=PACK)[:, lo:hi],
-                pieces[f, b, a][:].rearrange("p i (m t) -> p m i t", t=PACK)[:, lo:hi],
-            )
+            dst = woven["w", f, b, a][:].rearrange("p (t m i) -> p m i t", t=PACK, i=PACK)[:, lo:hi]
+            src = pieces[f, b, a][:].rearrange("p i (m t) -> p m i t", t=PACK)[:, lo:hi]
+            for first in range(0, PACK, slices_at_once):
+                cut = slice(first, first + slices_at_once)
+                copy(dst[:, :, :, cut], src[:, :, :, cut])
 
         def prepare_piece(f, b, a):
             codes = slot([P, W], U32, "wq%d%d%dc" % (f, b, a))
@@ -208,18 +214,16 @@ def tile_list_deformable_texture_energy_kernel(tc, xT, wgt, offs, we, wo, wd_wor
             return squares[f, b, lo // W][:, PACK * (lo % W) : PACK * (lo % W + width)]
 
         def square(f, b, key):
-            dst, src = squares_of(f, b, key, P), sums[f, b, key][:]
+            count = slices[b, key]
+            dst = squares_of(f, b, key, P).rearrange("p (j t) -> p j t", t=count)
+            src = sums[f, b, key][:].rearrange("p (t j) -> p j t", t=count)
             if b == 1 and (f, key) in SQUARED_ON_VECTOR:
-                twin = slot([P, W], F32, "twin", 2)
-                cuts = (slice(0, W // 2), slice(W // 2, W))
+                twin = slot([P, W // count, count], F32, "twin", 2)
+                cuts = (slice(0, W // count // 2), slice(W // count // 2, W // count))
                 for cut in cuts:
                     nc.vector.tensor_copy(twin[:, cut], src[:, cut])
                 for cut in cuts:
                     nc.vector.tensor_tensor(dst[:, cut], src[:, cut], twin[:, cut], ALU.mult)
-            elif slices[b, key] == PACK:
-                nc.scalar.activation(
-                    dst.rearrange("p (j t) -> p j t", t=PACK), src.rearrange("p (t j) -> p j t", t=PACK), ACT.Square
-                )
             else:
                 nc.scalar.activation(dst, src, ACT.Square)
 
@@ -253,15 +257,15 @@ def tile_list_deformable_texture_energy_kernel(tc, xT, wgt, offs, we, wo, wd_wor
 
         def add_squares(b, lo, width, tag):
             totals[b, lo] = slot([P, PACK * width], F32, tag)
-            nc.vector.tensor_tensor(totals[b, lo][:], squares_of(EVEN, b, lo, width), squares_of(ODD, b, lo, width), ALU.add)
+            count = slices[b, lo]
+            even, odd = (
+                squares_of(f, b, lo, width).rearrange("p (n j v) -> p j n v", n=PACK // count, v=count) for f in (EVEN, ODD)
+            )
+            nc.vector.tensor_tensor(totals[b, lo][:].rearrange("p (j n v) -> p j n v", n=PACK // count, v=count), even, odd, ALU.add)
 
         def root(b, lo, width):
             woven["h", b, lo] = slot([P, PACK * width], BF16, "h%d%d" % (b, lo))
-            dst, src = woven["h", b, lo][:], totals[b, lo][:]
-            if slices[b, lo] != PACK:
-                dst = dst.rearrange("p (c j t) -> p c t j", j=4, t=PACK)
-                src = src.rearrange("p (t c j) -> p c t j", j=4, t=PACK)
-            nc.scalar.activation(dst, src, ACT.Sqrt)
+            nc.scalar.activation(woven["h", b, lo][:], totals[b, lo][:], ACT.Sqrt)
 
         def quantise_h(b, lo):
             codes, scales = quantise(woven["h", b, lo], "hq%d%d" % (b, lo))
@@ -324,19 +328,19 @@ def tile_list_deformable_texture_energy_kernel(tc, xT, wgt, offs, we, wo, wd_wor
             load_piece(ODD, 1, a, "plane1%d" % a)
         wd_codes, bias_columns = load_last_stage()
 
-        weave_piece(EVEN, 0, 0, on_scalar)
+        weave_piece(EVEN, 0, 0, on_scalar, PACK)
         for lo in (0, QUARTER):
             gather(0, 1, PACK - 1, lo, QUARTER)
         for lo in (0, QUARTER):
             weave_x(0, 1, lo, QUARTER)
         quantise_piece(EVEN, 0, 0)
         gather(1, 1, PACK - 1)
-        weave_piece(EVEN, 0, 1, on_vector)
         weave_x(1, 1)
-        quantise_x(0, 1)
-        quantise_piece(EVEN, 0, 1)
-        weave_piece(ODD, 0, 0, on_vector, 0, P - SCALAR_GROUPS)
-        weave_piece(ODD, 0, 0, on_scalar, P - SCALAR_GROUPS, P)
+        quantise_x(0, 1, 0, QUARTER)
+        prepare_piece(EVEN, 0, 1)
+        quantise_x(0, 1, QUARTER, QUARTER)
+        weave_piece(ODD, 0, 0, on_vector, 2, 0, P - SCALAR_GROUPS)
+        weave_piece(ODD, 0, 0, on_scalar, PACK, P - SCALAR_GROUPS, P)
         quantise_x(1, 1)
         quantise_piece(ODD, 0, 0)
         prepare_piece(ODD, 0, 1)

@@ -215,11 +215,12 @@ def tile_list_deformable_texture_energy_kernel(tc, xT, wgt, offs, we, wo, wd_wor
 
         def square(f, b, key):
             count = slices[b, key]
-            dst = squares_of(f, b, key, P).rearrange("p (j t) -> p j t", t=count)
-            src = sums[f, b, key][:].rearrange("p (t j) -> p j t", t=count)
+            run = 2 if count == 2 else 1
+            dst = squares_of(f, b, key, P).rearrange("p (c j t) -> p c t j", j=run, t=count)
+            src = sums[f, b, key][:].rearrange("p (t c j) -> p c t j", j=run, t=count)
             if b == 1 and (f, key) in SQUARED_ON_VECTOR:
-                twin = slot([P, W // count, count], F32, "twin", 2)
-                cuts = (slice(0, W // count // 2), slice(W // count // 2, W // count))
+                twin = slot([P, W], F32, "twin", 2)[:].rearrange("p (c j t) -> p c t j", j=run, t=count)
+                cuts = (slice(0, dst.shape[1] // 2), slice(dst.shape[1] // 2, dst.shape[1]))
                 for cut in cuts:
                     nc.vector.tensor_copy(twin[:, cut], src[:, cut])
                 for cut in cuts:
@@ -250,8 +251,8 @@ def tile_list_deformable_texture_energy_kernel(tc, xT, wgt, offs, we, wo, wd_wor
             woven["h", b, lo] = slot([P, PACK * width], BF16, "h%d%d" % (b, lo))
             for at in range(lo, lo + width, P):
                 nc.scalar.activation(
-                    woven["h", b, lo][:, PACK * (at - lo) : PACK * (at - lo + P)].rearrange("p (j t) -> p j t", t=PACK),
-                    totals[b, at][:].rearrange("p t j -> p j t"),
+                    woven["h", b, lo][:, PACK * (at - lo) : PACK * (at - lo + P)].rearrange("p (c j t) -> p c t j", j=2, t=PACK),
+                    totals[b, at][:].rearrange("p t (c j) -> p c t j", j=2),
                     ACT.Sqrt,
                 )
 

@@ -32,6 +32,9 @@ PARTS = ((0, 256), (256, 256), (512, 256), (768, 128), (896, 128))
 SQUARED_ON_VECTOR = ((EVEN, 256), (EVEN, 640))
 SCALAR_GROUPS = 20
 PARTS_SHARED_WITH_SCALAR = 3
+WINDOWS = (1,)
+ON_GPSIMD = 512
+REGION = 8192
 
 
 def tile_list_deformable_texture_energy_kernel(tc, xT, wgt, offs, we, wo, wd_words, wd_scales, bias, out):
@@ -39,10 +42,14 @@ def tile_list_deformable_texture_energy_kernel(tc, xT, wgt, offs, we, wo, wd_wor
     with ExitStack() as ctx:
         lists = ctx.enter_context(tc.tile_pool(name="lists", bufs=1))
         keep = ctx.enter_context(tc.tile_pool(name="keep", bufs=1))
+        late = ctx.enter_context(tc.tile_pool(name="late", bufs=1))
         psum = ctx.enter_context(tc.psum_pool(name="psum", bufs=1))
 
         def slot(shape, dtype, tag, bufs=1):
             return keep.tile(shape, dtype, name=tag, tag=tag, bufs=bufs, align_bytes=64)
+
+        def placed(shape, dtype, name, offset):
+            return late.tile(shape, dtype, name=name, tag=name, offset=offset, align_bytes=64)
 
         banks_taken = []
 
@@ -66,6 +73,7 @@ def tile_list_deformable_texture_energy_kernel(tc, xT, wgt, offs, we, wo, wd_wor
         planes, gains, pieces, picked, woven = {}, {}, {}, {}, {}
         xq, wq, hq = {}, {}, {}
         sums, slices, squares, totals = {}, {}, {}, {}
+        in_banks = set()
 
         def load_gains():
             chunks = slot([P, CHUNK], F32, "chunks")
@@ -264,9 +272,34 @@ def tile_list_deformable_texture_energy_kernel(tc, xT, wgt, offs, we, wo, wd_wor
             )
             nc.vector.tensor_tensor(totals[b, lo][:].rearrange("p (j n v) -> p j n v", n=PACK // count, v=count), even, odd, ALU.add)
 
-        def root(b, lo, width):
-            woven["h", b, lo] = slot([P, PACK * width], BF16, "h%d%d" % (b, lo))
-            nc.scalar.activation(woven["h", b, lo][:], totals[b, lo][:], ACT.Sqrt)
+        def add_in_window(k):
+            lo, width = PARTS[k + 1]
+            totals[1, lo] = slot([P, PACK * width], F32, "plane03")
+            in_banks.add(lo)
+            even, odd = (squares_of(f, 1, lo, width) for f in (EVEN, ODD))
+            cut = slice(PACK * width - ON_GPSIMD, PACK * width)
+            nc.gpsimd.tensor_tensor(totals[1, lo][:, cut], even[:, cut], odd[:, cut], ALU.add)
+            return lo, width
+
+        def add_first_bank(lo, width):
+            even, odd = (squares_of(f, 1, lo, width) for f in (EVEN, ODD))
+            cut = slice(0, PACK * width - ON_GPSIMD)
+            nc.vector.tensor_tensor(totals[1, lo][:, cut], even[:, cut], odd[:, cut], ALU.add)
+
+        def root(b, lo, width, window=None):
+            if window is None:
+                woven["h", b, lo] = slot([P, PACK * width], BF16, "h%d%d" % (b, lo))
+            else:
+                woven["h", b, lo] = placed([P, PACK * width], BF16, "h%d%d" % (b, lo), REGION * window + 3 * REGION // 8)
+            if b == 1 and lo in in_banks:
+                count = slices[b, lo]
+                nc.scalar.activation(
+                    woven["h", b, lo][:].rearrange("p (j n v) -> p j n v", n=PACK // count, v=count),
+                    totals[b, lo][:].rearrange("p (n j v) -> p j n v", n=PACK // count, v=count),
+                    ACT.Sqrt,
+                )
+            else:
+                nc.scalar.activation(woven["h", b, lo][:], totals[b, lo][:], ACT.Sqrt)
 
         def quantise_h(b, lo):
             codes, scales = quantise(woven["h", b, lo], "hq%d%d" % (b, lo))
@@ -292,7 +325,7 @@ def tile_list_deformable_texture_energy_kernel(tc, xT, wgt, offs, we, wo, wd_wor
 
         def store(lo, width, n, by_scalar):
             acc = sums["out", lo, n]
-            result = slot([P, 2, width], F32, "result", 10)
+            result = slot([P, 2, width], F32, "result", 8)
             if by_scalar:
                 for v in range(2):
                     column = bias_columns[:, 2 * n + v : 2 * n + v + 1]
@@ -303,6 +336,16 @@ def tile_list_deformable_texture_energy_kernel(tc, xT, wgt, offs, we, wo, wd_wor
             rows = out[2 * P * n : 2 * P * (n + 1), lo : lo + width]
             queue = nc.scalar if by_scalar else nc.sync
             queue.dma_start(rows.rearrange("(v p) j -> p v j", p=P), result[:])
+
+        def store_in_window(k):
+            lo, width = PARTS[k - 1]
+            result = placed([P, N // P, width], F32, "results%d" % k, REGION * WINDOWS.index(k))
+            for n in range(2):
+                for v in range(2):
+                    u = 2 * n + v
+                    nc.vector.tensor_scalar_add(result[:, u, :], sums["out", lo, n][:, v, :], bias_columns[:, u : u + 1])
+                rows = out[2 * P * n : 2 * P * (n + 1), lo : lo + width]
+                nc.sync.dma_start(rows.rearrange("(v p) j -> p v j", p=P), result[:, 2 * n : 2 * n + 2, :])
 
         load_gains()
         load_plane(0, 0)
@@ -388,7 +431,8 @@ def tile_list_deformable_texture_energy_kernel(tc, xT, wgt, offs, we, wo, wd_wor
             for lo, width in PARTS[k : k + 1]:
                 root(1, lo, width)
             for lo, width in PARTS[k + 1 : k + 2]:
-                add_squares(1, lo, width, total_homes[k + 1])
+                if k not in WINDOWS:
+                    add_squares(1, lo, width, total_homes[k + 1])
             for lo, width in PARTS[k + 2 : k + 3]:
                 for f in (EVEN, ODD):
                     square_all(f, 1, lo, width)
@@ -397,7 +441,11 @@ def tile_list_deformable_texture_energy_kernel(tc, xT, wgt, offs, we, wo, wd_wor
                     quantise_h(0, lo)
                 quantise_h(1, lo)
                 project(lo, width)
-            if k > 0:
+            if k + 1 in WINDOWS:
+                pending = add_in_window(k + 1)
+                store_in_window(k + 1)
+                add_first_bank(*pending)
+            elif k > 0 and k not in WINDOWS:
                 lo, width = PARTS[k - 1]
                 for n in range(2):
                     store(lo, width, n, n == 1 and k > len(PARTS) - PARTS_SHARED_WITH_SCALAR)

@@ -69,6 +69,9 @@ def tile_list_deformable_texture_energy_kernel(tc, xT, wgt, offs, we, wo, wd_wor
         nc.vector.memset(warm[:, 0:1], 1.0)
         nc.scalar.activation(warm[:, 1:2], warm[:, 0:1], ACT.Sqrt)
 
+        warm_sum = slot([P, 8], F32, "warm_sum")
+        nc.gpsimd.tensor_tensor(warm_sum[:], identity[:, :8], identity[:, :8], ALU.add)
+
         on_scalar, on_vector = nc.scalar.copy, nc.vector.tensor_copy
         planes, gains, pieces, picked, woven = {}, {}, {}, {}, {}
         xq, wq, hq = {}, {}, {}

from contextlib import ExitStack

import concourse.mybir as mybir
from concourse.masks import make_identity

K, T, S, H, N = 1024, 2048, 1024, 1024, 512
FLOPS = 2 * (2 * K * H * S + H * N * S)

F32 = mybir.dt.float32
BF16 = mybir.dt.bfloat16
I32 = mybir.dt.int32
U32 = mybir.dt.uint32
U16 = mybir.dt.uint16
U8 = mybir.dt.uint8
FP8X4 = mybir.dt.float8_e4m3fn_x4
FP4X4 = mybir.dt.float4_e2m1fn_x4
ACT = mybir.ActivationFunctionType
ALU = mybir.AluOpType

P = 128
PACK = 4
KP = P * PACK
W = 512
BANKS = 8
QUAD = 32
HEAD = 16
CHUNK = S // HEAD
QUARTER = 256
EVEN, ODD = 0, 1

PARTS = ((0, 256), (256, 256), (512, 256), (768, 128), (896, 128))
SQUARED_ON_VECTOR = ((EVEN, 256), (EVEN, 640))
SCALAR_GROUPS = 20
PARTS_SHARED_WITH_SCALAR = 3
WINDOWS = (1,)
ON_GPSIMD = 512
REGION = 8192


def tile_list_deformable_texture_energy_kernel(tc, xT, wgt, offs, we, wo, wd_words, wd_scales, bias, out):
    nc = tc.nc
    with ExitStack() as ctx:
        lists = ctx.enter_context(tc.tile_pool(name="lists", bufs=1))
        keep = ctx.enter_context(tc.tile_pool(name="keep", bufs=1))
        late = ctx.enter_context(tc.tile_pool(name="late", bufs=1))
        psum = ctx.enter_context(tc.psum_pool(name="psum", bufs=1))

        def slot(shape, dtype, tag, bufs=1):
            return keep.tile(shape, dtype, name=tag, tag=tag, bufs=bufs, align_bytes=64)

        def placed(shape, dtype, name, offset):
            return late.tile(shape, dtype, name=name, tag=name, offset=offset, align_bytes=64)

        banks_taken = []

        def bank(shape):
            index = len(banks_taken) % BANKS
            banks_taken.append(index)
            return psum.tile(shape, F32, name="bank%d" % index, tag="bank%d" % index, bufs=1)

        offsets = lists.tile([P, S // HEAD], U16, name="offsets")

        wd_plane = slot([P, 2, N], U8, "wd_plane")
        nc.gpsimd.memset(wd_plane[:].rearrange("p a n -> p (a n)").bitcast(I32), 0)
        identity = slot([P, P], F32, "identity")
        make_identity(nc, identity[:])

        warm = slot([P, 2], F32, "warm")
        nc.vector.memset(warm[:, 0:1], 1.0)
        nc.scalar.activation(warm[:, 1:2], warm[:, 0:1], ACT.Sqrt)

        warm_sum = slot([P, 8], F32, "warm_sum")
        nc.gpsimd.tensor_tensor(warm_sum[:], identity[:, :8], identity[:, :8], ALU.add)

        on_scalar, on_vector = nc.scalar.copy, nc.vector.tensor_copy
        planes, gains, pieces, picked, woven = {}, {}, {}, {}, {}
        xq, wq, hq = {}, {}, {}
        sums, slices, squares, totals = {}, {}, {}, {}
        in_banks = set()

        def load_gains():
            chunks = slot([P, CHUNK], F32, "chunks")
            flat = wgt.rearrange("p j -> (p j)")
            for q in range(P // QUAD):
                first = QUAD * S * q + S
                rows = flat[first : first + QUAD * (S - CHUNK)].rearrange("(r s) -> r s", s=S - CHUNK)
                nc.sync.dma_start(chunks[QUAD * q : QUAD * (q + 1), :], rows[:, :CHUNK])
            turned = slot([P, CHUNK], F32, "turned")
            for e in range(CHUNK // QUAD):
                nc.vector.transpose(turned[:, QUAD * e : QUAD * (e + 1)], chunks[:, QUAD * e : QUAD * (e + 1)])
            by_source = turned[:].rearrange("p (e h c) -> p c e h", e=2, h=2).unsqueeze(4)
            for hf, runs in enumerate(
                (
                    ((0, 1, slice(0, 1), on_vector), (1, 8, slice(15, 8, -1), on_vector)),
                    ((0, 8, slice(8, 0, -1), on_vector),),
                )
            ):
                spread = slot([P, W], F32, "spread%d" % hf)
                by_chunk = spread[:].rearrange("p (k e h r) -> p k e h r", e=2, h=2, r=HEAD)
                for lo, hi, sources, copy in runs:
                    copy(by_chunk[:, lo:hi], by_source[:, sources].to_broadcast([P, hi - lo, 2, 2, HEAD]))
                gains[hf] = slot([P, W], F32, "gain%d" % hf)
                nc.vector.transpose(gains[hf][:], spread[:])

        def load_plane(a, i):
            planes[a, i] = slot([P, T], F32, "plane%d%d" % (a, i))
            rows = xT[KP * a : KP * (a + 1), :].rearrange("(p i) t -> p i t", i=PACK)
            nc.sync.dma_start(planes[a, i][:], rows[:, i, :])

        def load_piece(f, b, a, tag):
            pieces[f, b, a] = slot([P, PACK, W], F32, tag)
            rows = (we, wo)[f][KP * a : KP * (a + 1), W * b : W * (b + 1)]
            nc.sync.dma_start(pieces[f, b, a][:], rows.rearrange("(p i) c -> p i c", i=PACK))

        def load_last_stage():
            words = slot([P, 2, 2 * N], U8, "wd_words")
            nc.sync.dma_start(words[:].bitcast(I32), wd_words.rearrange("a p c -> p a c").bitcast(I32))
            for q in range(P // QUAD):
                nc.sync.dma_start(
                    wd_plane[QUAD * q : QUAD * q + 4, :, :].bitcast(I32),
                    wd_scales[:, 4 * q : 4 * q + 4, :].rearrange("a r n -> r a n").bitcast(I32),
                )
            columns = slot([P, N // P], F32, "bias_columns")
            with nc.allow_non_contiguous_dma(reason="one bias value a partition"):
                nc.sync.dma_start(columns[:], bias.rearrange("(u p) -> p u", p=P))
            return words, columns

        def quantise(values, name):
            width = values.shape[1] // PACK
            codes = slot([P, width], U32, name + "c")
            scales = slot([P, width], U8, name + "s")
            nc.vector.quantize_mx(out=codes[:].bitcast(FP8X4), scales=scales[:], in_=values[:])
            return codes, scales

        def gather(hf, a, i, lo=0, width=W):
            if (i, lo) == (0, 0):
                picked[hf, a] = slot([P, PACK, W], F32, "picked%d%d" % (hf, a))
            cut = offsets[:, (hf * W + lo) // HEAD : (hf * W + lo + width) // HEAD]
            nc.vector.tensor_tensor(
                picked[hf, a][:, i, lo : lo + width], planes[a, i][:].indirect(cut), gains[hf][:, lo : lo + width], ALU.mult
            )

        def weave_x(hf, a, lo=0, width=W):
            if lo == 0:
                woven["x", hf, a] = slot([P, PACK * W], BF16, "woven_x", 2)
            on_scalar(
                woven["x", hf, a][:, PACK * lo : PACK * (lo + width)].rearrange("p (c j i) -> p c i j", j=4, i=PACK),
                picked[hf, a][:, :, lo : lo + width].rearrange("p i (c j) -> p c i j", j=4),
            )

        def quantise_x(hf, a, lo=0, width=W):
            if lo == 0:
                xq[hf, a] = (slot([P, W], U32, "xq%d%dc" % (hf, a)), slot([P, W], U8, "xq%d%ds" % (hf, a)))
            codes, scales = xq[hf, a]
            values = woven["x", hf, a][:, PACK * lo : PACK * (lo + width)]
            cut = slice(lo, lo + width)
            nc.vector.quantize_mx(out=codes[:, cut].bitcast(FP8X4), scales=scales[:, cut], in_=values)

        def weave_piece(f, b, a, copy, slices_at_once, lo=0, hi=P):
            if lo == 0:
                woven["w", f, b, a] = slot([P, PACK * W], BF16, "woven_w", 3)
            dst = woven["w", f, b, a][:].rearrange("p (t m i) -> p m i t", t=PACK, i=PACK)[:, lo:hi]
            src = pieces[f, b, a][:].rearrange("p i (m t) -> p m i t", t=PACK)[:, lo:hi]
            for first in range(0, PACK, slices_at_once):
                cut = slice(first, first + slices_at_once)
                copy(dst[:, :, :, cut], src[:, :, :, cut])

        def prepare_piece(f, b, a):
            codes = slot([P, W], U32, "wq%d%d%dc" % (f, b, a))
            scales = slot([P, W], U8, "wq%d%d%ds" % (f, b, a))
            wq[f, b, a] = (codes, scales)
            halves = [slot([P, 2 * W], BF16, "woven_half", 4) for u in range(2)]
            for u in range(2):
                on_vector(
                    halves[u][:].rearrange("p (t m i) -> p m i t", t=2, i=PACK),
                    pieces[f, b, a][:].rearrange("p i (m t) -> p m i t", t=PACK)[:, :, :, 2 * u : 2 * u + 2],
                )
            for u in range(2):
                cut = slice(2 * P * u, 2 * P * (u + 1))
                nc.vector.quantize_mx(out=codes[:, cut].bitcast(FP8X4), scales=scales[:, cut], in_=halves[u][:])

        def quantise_piece(f, b, a):
            wq[f, b, a] = quantise(woven["w", f, b, a], "wq%d%d%d" % (f, b, a))

        def mx_pass(acc, stationary, at, moving, lo, width, start, stop):
            nc.tensor.matmul_mx(
                acc,
                lhsT=stationary[0][:, at : at + P].bitcast(FP8X4),
                lhsT_scale=stationary[1][:, at : at + P],
                rhs=moving[0][:, lo : lo + width].bitcast(FP8X4),
                rhs_scale=moving[1][:, lo : lo + width],
                start=start,
                stop=stop,
            )

        def respond_by_query(f, b, lo, width, passes=(0, 1)):
            for at in range(lo, lo + width, P):
                for a in passes:
                    if a == 0:
                        sums[f, b, at] = bank([P, W])
                        slices[b, at] = 1
                    mx_pass(sums[f, b, at][:], xq[at // W, a], at % W, wq[f, b, a], 0, W, a == 0, a == 1)

        def respond_by_filter(f, b, lo, width, passes=(0, 1)):
            per_bank = W // width
            for n in range(PACK // per_bank):
                key = lo + P * n
                for a in passes:
                    if a == 0:
                        sums[f, b, key] = bank([P, W])
                        slices[b, key] = per_bank
                    for v in range(per_bank):
                        mx_pass(
                            sums[f, b, key][:, width * v : width * (v + 1)],
                            wq[f, b, a],
                            P * (per_bank * n + v),
                            xq[lo // W, a],
                            lo % W,
                            width,
                            (a, v) == (0, 0),
                            (a, v) == (1, per_bank - 1),
                        )

        def squares_of(f, b, lo, width):
            return squares[f, b, lo // W][:, PACK * (lo % W) : PACK * (lo % W + width)]

        def square(f, b, key):
            count = slices[b, key]
            run = 2 if count == 2 else 1
            dst = squares_of(f, b, key, P).rearrange("p (c j t) -> p c t j", j=run, t=count)
            src = sums[f, b, key][:].rearrange("p (t c j) -> p c t j", j=run, t=count)
            if b == 1 and (f, key) in SQUARED_ON_VECTOR:
                twin = slot([P, W], F32, "twin", 2)[:].rearrange("p (c j t) -> p c t j", j=run, t=count)
                cuts = (slice(0, dst.shape[1] // 2), slice(dst.shape[1] // 2, dst.shape[1]))
                for cut in cuts:
                    nc.vector.tensor_copy(twin[:, cut], src[:, cut])
                for cut in cuts:
                    nc.vector.tensor_tensor(dst[:, cut], src[:, cut], twin[:, cut], ALU.mult)
            else:
                nc.scalar.activation(dst, src, ACT.Square)

        def square_all(f, b, lo, width):
            keys = range(lo, lo + width, P)
            for key in sorted(keys, key=lambda k: (b, (f, k) in SQUARED_ON_VECTOR) != (1, True)):
                square(f, b, key)

        def turn_and_add(b, lo, width):
            for at in range(lo, lo + width, P):
                totals[b, at] = bank([P, PACK, P])
                for t in range(PACK):
                    for f in (EVEN, ODD):
                        nc.tensor.matmul(
                            totals[b, at][:, t, :],
                            lhsT=squares_of(f, b, at, P)[:, P * t : P * (t + 1)],
                            rhs=identity[:],
                            start=(f == EVEN),
                            stop=(f == ODD),
                            is_transpose=True,
                        )

        def root_of_banks(b, lo, width):
            woven["h", b, lo] = slot([P, PACK * width], BF16, "h%d%d" % (b, lo))
            for at in range(lo, lo + width, P):
                nc.scalar.activation(
                    woven["h", b, lo][:, PACK * (at - lo) : PACK * (at - lo + P)].rearrange("p (c j t) -> p c t j", j=2, t=PACK),
                    totals[b, at][:].rearrange("p t (c j) -> p c t j", j=2),
                    ACT.Sqrt,
                )

        def add_squares(b, lo, width, tag):
            totals[b, lo] = slot([P, PACK * width], F32, tag)
            count = slices[b, lo]
            even, odd = (
                squares_of(f, b, lo, width).rearrange("p (n j v) -> p j n v", n=PACK // count, v=count) for f in (EVEN, ODD)
            )
            nc.vector.tensor_tensor(totals[b, lo][:].rearrange("p (j n v) -> p j n v", n=PACK // count, v=count), even, odd, ALU.add)

        def add_in_window(k):
            lo, width = PARTS[k + 1]
            totals[1, lo] = slot([P, PACK * width], F32, "plane03")
            in_banks.add(lo)
            even, odd = (squares_of(f, 1, lo, width) for f in (EVEN, ODD))
            cut = slice(PACK * width - ON_GPSIMD, PACK * width)
            nc.gpsimd.tensor_tensor(totals[1, lo][:, cut], even[:, cut], odd[:, cut], ALU.add)
            return lo, width

        def add_first_bank(lo, width):
            even, odd = (squares_of(f, 1, lo, width) for f in (EVEN, ODD))
            cut = slice(0, PACK * width - ON_GPSIMD)
            nc.vector.tensor_tensor(totals[1, lo][:, cut], even[:, cut], odd[:, cut], ALU.add)

        def root(b, lo, width, window=None):
            if window is None:
                woven["h", b, lo] = slot([P, PACK * width], BF16, "h%d%d" % (b, lo))
            else:
                woven["h", b, lo] = placed([P, PACK * width], BF16, "h%d%d" % (b, lo), REGION * window + 3 * REGION // 8)
            if b == 1 and lo in in_banks:
                count = slices[b, lo]
                nc.scalar.activation(
                    woven["h", b, lo][:].rearrange("p (j n v) -> p j n v", n=PACK // count, v=count),
                    totals[b, lo][:].rearrange("p (n j v) -> p j n v", n=PACK // count, v=count),
                    ACT.Sqrt,
                )
            else:
                nc.scalar.activation(woven["h", b, lo][:], totals[b, lo][:], ACT.Sqrt)

        def quantise_h(b, lo):
            codes, scales = quantise(woven["h", b, lo], "hq%d%d" % (b, lo))
            for at in range(0, codes.shape[1], P):
                hq[b, lo + at] = (codes, scales, at)

        def project(lo, width):
            for n in range(2):
                sums["out", lo, n] = bank([P, 2, width])
                for b in range(2):
                    codes, scales, at = hq[b, lo]
                    for v in range(2):
                        u = 2 * n + v
                        nc.tensor.matmul_mx(
                            sums["out", lo, n][:, v, :],
                            lhsT=wd_codes[:, b, 2 * P * u : 2 * P * (u + 1)].bitcast(FP4X4),
                            lhsT_scale=wd_plane[:, b, P * u : P * (u + 1)],
                            rhs=codes[:, at : at + width].bitcast(FP8X4),
                            rhs_scale=scales[:, at : at + width],
                            start=((b, v) == (0, 0)),
                            stop=((b, v) == (1, 1)),
                        )

        def store(lo, width, n, by_scalar):
            acc = sums["out", lo, n]
            result = slot([P, 2, width], F32, "result", 8)
            if by_scalar:
                for v in range(2):
                    column = bias_columns[:, 2 * n + v : 2 * n + v + 1]
                    nc.scalar.activation(result[:, v, :], acc[:, v, :], ACT.Identity, bias=column)
            else:
                columns = bias_columns[:, 2 * n : 2 * n + 2].unsqueeze(2)
                nc.vector.tensor_tensor(result[:], acc[:], columns.to_broadcast([P, 2, width]), ALU.add)
            rows = out[2 * P * n : 2 * P * (n + 1), lo : lo + width]
            queue = nc.scalar if by_scalar else nc.sync
            queue.dma_start(rows.rearrange("(v p) j -> p v j", p=P), result[:])

        def store_in_window(k):
            lo, width = PARTS[k - 1]
            result = placed([P, N // P, width], F32, "results%d" % k, REGION * WINDOWS.index(k))
            for n in range(2):
                for v in range(2):
                    u = 2 * n + v
                    nc.vector.tensor_scalar_add(result[:, u, :], sums["out", lo, n][:, v, :], bias_columns[:, u : u + 1])
                rows = out[2 * P * n : 2 * P * (n + 1), lo : lo + width]
                nc.sync.dma_start(rows.rearrange("(v p) j -> p v j", p=P), result[:, 2 * n : 2 * n + 2, :])

        load_gains()
        load_plane(0, 0)
        nc.sync.dma_start(offsets[:], offs)
        for a, i in [(a, i) for a in range(2) for i in range(PACK)][1:-1]:
            load_plane(a, i)
        load_piece(EVEN, 0, 0, "first")
        load_plane(1, PACK - 1)
        load_piece(EVEN, 0, 1, "second")

        for i in range(PACK):
            for hf in range(2):
                gather(hf, 0, i)
        for i, (f, b, a) in enumerate(((ODD, 0, 0), (ODD, 0, 1), (EVEN, 1, 0), (EVEN, 1, 1))):
            load_piece(f, b, a, "plane0%d" % i)
        for hf in range(2):
            weave_x(hf, 0)
        for i in range(PACK - 1):
            for hf in range(2):
                gather(hf, 1, i)
            if i < 2:
                quantise_x(i, 0)
        for a in range(2):
            load_piece(ODD, 1, a, "plane1%d" % a)
        wd_codes, bias_columns = load_last_stage()

        weave_piece(EVEN, 0, 0, on_scalar, PACK)
        for lo in (0, QUARTER):
            gather(0, 1, PACK - 1, lo, QUARTER)
        for lo in (0, QUARTER):
            weave_x(0, 1, lo, QUARTER)
        quantise_piece(EVEN, 0, 0)
        gather(1, 1, PACK - 1)
        weave_x(1, 1)
        quantise_x(0, 1, 0, QUARTER)
        prepare_piece(EVEN, 0, 1)
        quantise_x(0, 1, QUARTER, QUARTER)
        weave_piece(ODD, 0, 0, on_vector, 2, 0, P - SCALAR_GROUPS)
        weave_piece(ODD, 0, 0, on_scalar, PACK, P - SCALAR_GROUPS, P)
        quantise_x(1, 1)
        quantise_piece(ODD, 0, 0)
        prepare_piece(ODD, 0, 1)

        homes = (("picked00", "picked10", "first", "plane12"), ("plane13", "picked01", "picked11", "second"))
        for b in range(2):
            for f in (EVEN, ODD):
                for hf in range(2):
                    squares[f, b, hf] = slot([P, PACK * W], F32, homes[b][2 * f + hf])

        for a in range(2):
            respond_by_filter(EVEN, 0, 0, QUARTER, (a,))
            respond_by_query(EVEN, 0, QUARTER, S - QUARTER, (a,))
        square_all(EVEN, 0, 0, S)
        for a in range(2):
            respond_by_filter(ODD, 0, 0, QUARTER, (a,))
            respond_by_query(ODD, 0, QUARTER, QUARTER, (a,))
        respond_by_query(ODD, 0, W, W)
        square_all(ODD, 0, 0, S)
        prepare_piece(EVEN, 1, 0)
        add_squares(0, 0, QUARTER, "plane00")
        prepare_piece(EVEN, 1, 1)
        root(0, 0, QUARTER)
        turn_and_add(0, QUARTER, S - QUARTER)
        for lo in range(QUARTER, S, QUARTER):
            root_of_banks(0, lo, QUARTER)
        prepare_piece(ODD, 1, 0)
        quantise_h(0, 0)
        prepare_piece(ODD, 1, 1)
        quantise_h(0, QUARTER)

        total_homes = ("plane01", "plane02", "plane03", "plane10", "plane11")
        for step in (respond_by_filter, square_all):
            for f in (EVEN, ODD):
                for lo, width in PARTS[:2]:
                    step(f, 1, lo, width)
        for f in (EVEN, ODD):
            respond_by_filter(f, 1, *PARTS[2])
        add_squares(1, *PARTS[0], total_homes[0])
        for k in range(len(PARTS) + 1):
            for lo, width in PARTS[k + 3 : k + 4]:
                for f in (EVEN, ODD):
                    respond_by_filter(f, 1, lo, width)
            for lo, width in PARTS[k : k + 1]:
                root(1, lo, width)
            for lo, width in PARTS[k + 1 : k + 2]:
                if k not in WINDOWS:
                    add_squares(1, lo, width, total_homes[k + 1])
            for lo, width in PARTS[k + 2 : k + 3]:
                for f in (EVEN, ODD):
                    square_all(f, 1, lo, width)
            for lo, width in PARTS[k : k + 1]:
                if (0, lo) not in hq:
                    quantise_h(0, lo)
                quantise_h(1, lo)
                project(lo, width)
            if k + 1 in WINDOWS:
                pending = add_in_window(k + 1)
                store_in_window(k + 1)
                add_first_bank(*pending)
            elif k > 0 and k not in WINDOWS:
                lo, width = PARTS[k - 1]
                for n in range(2):
                    store(lo, width, n, n == 1 and k > len(PARTS) - PARTS_SHARED_WITH_SCALAR)
